import numpy as np, ml_dtypes
CORES = [3,11,19,27,35,43]
N = 6
BF = ml_dtypes.bfloat16
def gentries(a):
    return np.ascontiguousarray(a.reshape(8, 16, -1).transpose(0, 2, 1)).reshape(8, -1)
def gtable(e):
    e = np.asarray(e); return np.ascontiguousarray(e.reshape(8, -1, 16).transpose(0, 2, 1)).reshape(128, -1).astype(np.int32)
P, S, C, R = 2048, 80, 96, 3
def members(v):
    return np.stack([gentries(u) for u in v]).reshape(N, 8, R, N, C)
def pack(x, w, a, b):
    return {"fld": x.reshape(N, 128, P).astype(np.float32).astype(BF), "law": w.reshape(N, 128, S * S).astype(np.float32).astype(BF),
            "la": np.stack([gtable(u.reshape(8, -1)) for u in a]), "lb": np.stack([gtable(u.reshape(8, -1)) for u in b])}
def cut(p):
    return p[..., :N * C].reshape(N, 8, R, N, C), p[..., N * C:2 * N * C].reshape(N, 8, R, N, C)
def raw(rng):
    x = rng.integers(-128, 129, (N, 8, 16, P)); x[:, :, 0] = rng.integers(0, S, (N, 8, P))
    w = rng.integers(-16, 17, (N, 8, 16, S * S)); w[:, :, :2] = rng.integers(0, S, (N, 8, 2, S * S))
    a, b = cut(rng.permuted(np.tile(np.arange(P), (N, 8, R, 1)), axis=-1))
    return x, w, a, b
def setup_inputs(rng):
    return pack(*raw(rng))
def setup_inputs_swap(rng):
    x, w, a, b = raw(rng); a2, b2 = a.copy(), b.copy()
    for t in range(R):
        a2[:, :, t], b2[:, :, t] = (a[:, :, 0], b[:, :, 0]) if t % 2 == 0 else (b[:, :, 0], a[:, :, 0])
    return pack(x, w, a2, b2)
def setup_inputs_ends(rng):
    x, w, a, b = raw(rng); x[:, :, 0] = (S - 1) * rng.integers(0, 2, (N, 8, P)); w[:, :, :2] = (S - 1) * rng.integers(0, 2, (N, 8, 2, S * S))
    x[:, :, 1:] = 256 * rng.integers(0, 2, (N, 8, 15, P)) - 128; w[:, :, 2:] = 32 * rng.integers(0, 2, (N, 8, 14, S * S)) - 16
    w[:, :, 2::2] = 32 * rng.integers(0, 2, (N, 8, 7, 1)) - 16
    p = np.concatenate([np.arange(N * C), np.arange(P)[::-1][:N * C]])
    a, b = cut(np.tile(p, (N, 8, R, 1))); return pack(x, w, a, b)
def setup_inputs_one(rng):
    x, w, a, b = raw(rng); x[:, :, 0] = rng.integers(0, S, (N, 8, 1)); return pack(x, w, a, b)
def setup_inputs_spread(rng):
    x, w, a, b = raw(rng)
    x[:, :, 0] = np.floor(S * rng.random((N, 8, P)) ** 3); w[:, :, :2] = np.floor(S * rng.random((N, 8, 2, S * S)) ** 3)
    x[:, :, 1:] = np.floor(np.exp2(7 * rng.random((N, 8, 15, P)))) * rng.choice(np.array([-1, 0, 1]), (N, 8, 15, P))
    w[:, :, 2:] = np.floor(np.exp2(4 * rng.random((N, 8, 14, S * S)))) * rng.choice(np.array([-1, 0, 0, 1]), (N, 8, 14, S * S))
    a, b = cut(np.argsort(rng.random((N, 8, R, P)) + 2 * rng.random((N, 8, 1, P)), axis=-1)); return pack(x, w, a, b)
def check_inputs(d):
    bad = []; x = np.asarray(d["fld"]).astype(np.float32).reshape(N, 8, 16, P); w = np.asarray(d["law"]).astype(np.float32).reshape(N, 8, 16, S * S)
    if not ((x == np.floor(x)).all() and (x[:, :, 0] >= 0).all() and (x[:, :, 0] < S).all() and (np.abs(x[:, :, 1:]) <= 128).all()): bad.append("fields")
    if not ((w == np.floor(w)).all() and (w[:, :, :2] >= 0).all() and (w[:, :, :2] < S).all() and (np.abs(w[:, :, 2:]) <= 16).all()): bad.append("law")
    e = np.sort(np.concatenate([members(d["la"]).reshape(N, 8, R, N * C), members(d["lb"]).reshape(N, 8, R, N * C)], -1), -1)
    if not ((e >= 0).all() and (e < P).all()): bad.append("range")
    if not (e[..., 1:] > e[..., :-1]).all(): bad.append("disjoint")
    return bad
def reference(fld, law, la, lb):
    x = fld.astype(np.float32).astype(np.int64).reshape(N, 8, 16, P); w = law.astype(np.float32).astype(np.int64).reshape(N, 8, 16, S * S)
    a, b = members(la), members(lb)
    for t in range(R):
        for r in range(N):
            for q in range(N):
                for g in range(8):
                    u, v = x[r, g], x[q, g]; i, j = a[r, g, t, q], b[q, g, t, r]
                    col = w[r, g][:, u[0, i] * S + v[0, j]]
                    u[0, i] = col[0]; v[0, j] = col[1]
                    u[2:, i] += col[2:]; v[2:, j] -= col[2:]
    return {"y": x.reshape(N, 128, P).astype(np.float32)}

@@ -1,0 +1,281 @@
+from concourse.bass import DstId, RemoteDMATransfer
+from concourse.mybir import AluOpType, ActivationFunctionType
+
+N, P, S, C, R = 6, 2048, 80, 96, 3
+M = N * C
+W = M // 16
+H = M // 2
+SLOT = 40
+EARLY = 480
+LAW_A = 4480
+CHUNKS = [(0, 512), (512, 1024), (1024, 1536), (1536, 2048)]
+
+SCRATCH = {
+    "V": ("sbuf", [128, P + R * 2 * M], "bfloat16"),
+    "LAW": ("sbuf", [128, S * S], "bfloat16"),
+    "LA": ("sbuf", [128, R * W], "int32"),
+    "LB": ("sbuf", [128, R * W], "int32"),
+    "U0": ("sbuf", [128, 2 * R * W], "uint16"),
+    "TB": ("sbuf", [128, P], "float32"),
+    "RAMP": ("sbuf", [128, M], "float32"),
+    "ONES": ("sbuf", [128, 144], "bfloat16"),
+    "E1": ("sbuf", [128, 144], "bfloat16"),
+    "E80": ("sbuf", [128, 144], "bfloat16"),
+    "EF": ("sbuf", [128, 144], "float32"),
+    "ID": ("sbuf", [128, 128], "bfloat16"),
+    "PM": ("sbuf", [128, 128], "bfloat16"),
+    "P1": ("sbuf", [128, 128], "bfloat16"),
+    "P2": ("sbuf", [128, 128], "bfloat16"),
+    "PIDX": ("sbuf", [128, 4], "int32"),
+    "PA": ("sbuf", [128, 4], "int32"),
+    "NPA": ("sbuf", [128, 4], "float32"),
+    "IW0": ("sbuf", [128, 128], "float32"),
+    "IW": ("sbuf", [128, 128], "float32"),
+    "X": ("sbuf", [128, R * 2 * M], "bfloat16"),
+    "LV": ("sbuf", [128, R * N, SLOT], "bfloat16"),
+    "IDX": ("sbuf", [128, R * W + 4], "uint16"),
+    "COL": ("sbuf", [128, R * M], "bfloat16"),
+    "LD": ("sbuf", [128, R * M], "bfloat16"),
+    "PF": ("sbuf", [128, (R - 1) * 2 * M], "float32"),
+    "PI": ("sbuf", [128, (R - 1) * 2 * W + P // 16], "float32"),
+    "UP": ("sbuf", [128, (R - 1) * 2 * W + P // 16], "uint16"),
+    "Y": ("sbuf", [128, P], "float32"),
+}
+for _b in range(7):
+    SCRATCH["B%d" % _b] = ("psum", [128, 512], "float32")
+SEMAPHORES = ["left"] + ["one%d" % t for t in range(R)] + ["two%d" % t for t in range(R)] + ["s%d" % k for k in range(110)]
+
+
+def shared_engines(topo, src, dsts):
+    eng = [e for e in topo.engines(src, dsts[0]) if all(e in topo.engines(src, d) for d in dsts)]
+    n = 1
+    while 2 * n <= len(eng):
+        n *= 2
+    return eng[:n]
+
+
+def bits(eng):
+    return sum(1 << e for e in eng)
+
+
+def step_two_calls(topo, cores, r):
+    def far(q):
+        a, b = topo.chip(cores[r]), topo.chip(cores[q])
+        return 0 if a == b else 1 if topo.mates(a, b) else 2 if topo.same_plane(a, b) else 3
+    others = sorted([q for q in range(N) if q != r], key=lambda q: (-far(q), (q - r) % N))
+    eng = shared_engines(topo, cores[r], [cores[q] for q in others])
+    first = others[:-1]
+    each = len(eng) // len(first)
+    return [[(q, eng[i * each:(i + 1) * each]) for i, q in enumerate(first)], [(others[-1], eng)]]
+
+
+def rank_program(g, core, T, topo):
+    r = T.rank_of(core)
+    if r is None:
+        return
+    cores = list(T.cores)
+    A, F = AluOpType, ActivationFunctionType
+    ve, ac, pe, sy = g.vector, g.scalar, g.tensor, g.sync
+    queue = {"g": g, "ve": ve, "ac": ac, "pe": pe, "sy": sy}
+    total, seen, count = {}, {}, [0]
+
+    def new():
+        name = "s%d" % count[0]
+        count[0] += 1
+        total[name] = 0
+        return name
+
+    def sig(ins, ev=None, n=1):
+        ev = new() if ev is None else ev
+        assert ev not in seen
+        ins.then_inc(T.sem[ev], n)
+        total[ev] += n
+        return ev
+
+    def wait(q, *evs):
+        for ev in evs:
+            if q not in seen.setdefault(ev, []):
+                seen[ev].append(q)
+                queue[q].wait_ge(T.sem[ev], total[ev])
+
+    def dst_id(q):
+        rid, pid, _ = topo.addr(cores[q])
+        return DstId(rid=rid, pnc=pid)
+
+    others = [q for q in range(N) if q != r]
+    eng_one = shared_engines(topo, core, [cores[q] for q in others])
+    calls_two = step_two_calls(topo, cores, r)
+    total["left"] = 0
+    for t in range(R):
+        total["one%d" % t] = sum(len(shared_engines(topo, cores[s], [cores[q] for q in range(N) if q != s])) for s in others)
+        total["two%d" % t] = sum(len(e) for s in others for call in step_two_calls(topo, cores, s) for q, e in call if q == r)
+    B = [T["B%d" % b] for b in range(7)]
+
+    def wrap(out, sel, src, lo, hi, start, stop):
+        for k in range(16):
+            ins = pe.matmul(out, sel[:, 16 - k:144 - k], src[:, lo + k:hi:16], start and k == 0, stop and k == 15)
+        return ins
+
+    e_lb = sig(ac.dma_start(T.LB[:], T.lb[:]), n=16)
+    e_la = sig(ac.dma_start(T.LA[:], T.la[:]), n=16)
+    e_fld = sig(sy.dma_start(T.V[:, 0:P], T.fld[:]), n=16)
+    e_law = sig(sy.dma_start(T.LAW[:, 0:LAW_A], T.law[:, 0:LAW_A]), n=16)
+
+    e_ones = sig(ve.memset(T.ONES[:], 1.0))
+    e_tb = sig(ve.memset(T.TB[:], 0.0))
+    wait("g", e_ones)
+    e_e1 = sig(g.affine_select(T.E1[:], T.ONES[:], [[16, 9], [1001, 16]], A.is_equal, 0.0, -16, -1))
+    e_id = sig(g.affine_select(T.ID[:], T.ONES[:, 0:128], [[1, 128]], A.is_equal, 0.0, 0, -1))
+    e_ramp = sig(g.iota(T.RAMP[:], [[1, M]], 0, 0, allow_small_or_imprecise_dtypes=True))
+    e_pidx = sig(g.iota(T.PIDX[:, 0:1], [[1, 1]], 0, 1))
+    wait("g", e_id)
+    e_pm = sig(g.affine_select(T.PM[:], T.ID[:], [[0, 8], [1, 16]], A.not_equal, 0.0, 0, 0))
+    wait("ac", e_e1)
+    e_e80 = sig(ac.activation(T.E80[:], T.E1[:], F.Copy, scale=float(S)))
+    e_ef = sig(ac.activation(T.EF[:], T.E1[:], F.Copy))
+    wait("ve", e_lb)
+    e_ub = sig(ve.tensor_copy(T.U0[:, R * W:2 * R * W], T.LB[:]))
+    wait("ve", e_la)
+    e_ua = sig(ve.tensor_copy(T.U0[:, 0:R * W], T.LA[:]))
+
+    last_scatter = [e_tb]
+
+    def scatter(t, side, lo, hi):
+        c0 = side * R * W + t * W
+        wait("ve", last_scatter[0], e_ramp)
+        last_scatter[0] = sig(ve.tensor_scalar(T.TB[:, 0:P].indirect(T.U0[:, c0 + lo // 16:c0 + hi // 16]), T.RAMP[:, lo:hi],
+                                               1.0, float(P + 2 * M * t + side * M), A.mult, A.add))
+
+    ready = None
+    late = {}
+    for t in range(R):
+        win = T.V[:, 0:P + 2 * M * t]
+        xa, xb, c0, v0 = 2 * M * t, 2 * M * t + M, M * t, P + 2 * M * t
+        if t == 0:
+            off, oa, ob = T.U0, 0, R * W
+            wait("ve", e_ub, e_fld)
+            wait("ac", e_ub, e_fld)
+        else:
+            off, oa, ob = T.UP, 2 * W * (t - 1), 2 * W * (t - 1) + W
+            wait("ve", ready)
+            wait("ac", ready)
+        e_xb = sig(ve.tensor_copy(T.X[:, xb:xb + H], win.indirect(off[:, ob:ob + W // 2])))
+        sig(ac.activation(T.X[:, xb + H:xb + M], win.indirect(off[:, ob + W // 2:ob + W]), F.Copy), e_xb)
+        wait("pe", e_e1, e_xb)
+        e_vw = sig(wrap(B[1][:, 0:W], T.E1, T.X, xb, xb + M, True, True))
+        wait("ac", e_vw)
+        mine = T.LV[:, N * t + r, 0:W]
+        e_pay = sig(ac.activation(mine, B[1][:, 0:W], F.Copy))
+        wait("g", e_pay)
+        g.remote_dma_fused([RemoteDMATransfer(dst_ids=[dst_id(q) for q in others], dma_engine_mask=bits(eng_one),
+                                              remote_sem=T.sem["one%d" % t], srcs=[mine], dsts=[mine for q in others])],
+                           local_sem=T.sem.left)
+        total["left"] += len(eng_one)
+        if t == 0:
+            wait("sy", e_pay)
+            sig(sy.dma_start(T.LAW[:, LAW_A:S * S], T.law[:, LAW_A:S * S]), e_law, 16)
+            late["p1"] = sig(g.affine_select(T.P1[:], T.ID[:], [[0, 8], [1, 16]], A.not_equal, 0.0, -1, 0))
+            e = sig(g.affine_select(T.P2[:], T.ID[:], [[1, 128]], A.not_equal, -1.0, 0, -1))
+            wait("g", e)
+            e = sig(g.affine_select(T.P2[:], T.P2[:], [[0, 8], [1, 16]], A.is_ge, 0.0, -2, 0))
+            wait("g", e)
+            late["p2"] = sig(g.affine_select(T.P2[:], T.P2[:], [[16, 8], [1001, 16]], A.not_equal, 1.0, 1, -1))
+            late["iw0"] = sig(g.iota(T.IW0[:], [[16, 128]], 0, 1, allow_small_or_imprecise_dtypes=True))
+            wait("ve", e_ua)
+            wait("ac", e_ua)
+        scatter(t, 0, EARLY if t else 0, M)
+        scatter(t, 1, 0, M)
+        if t == 1:
+            wait("ve", e_pidx)
+            e = sig(ve.tensor_scalar(T.PA[:, 0:1], T.PIDX[:, 0:1], 128 - 16, None, A.bitwise_and))
+            wait("ve", e)
+            late["npa"] = sig(ve.tensor_scalar(T.NPA[:, 0:1], T.PA[:, 0:1], -1.0, None, A.mult))
+        e_xa = sig(ac.activation(T.X[:, xa:xa + M], win.indirect(off[:, oa:oa + W]), F.Copy))
+        if t == 2:
+            wait("ac", late["npa"], late["iw0"])
+            late["iw"] = sig(ac.activation(T.IW[:], T.IW0[:], F.Identity, bias=T.NPA[:, 0:1]))
+        wait("pe", e_pm, e_e80, e_id)
+        for h in range(2):
+            pe.matmul(B[4 + h][:, 0:H], T.PM[:], T.X[:, xb + h * H:xb + (h + 1) * H], True, False)
+        wait("pe", e_xa)
+        wrap(B[0][:, 0:W], T.E80, T.X, xa, xa + M, True, False)
+        for h in range(2):
+            pe.matmul(B[2 + h][:, 0:H], T.PM[:], T.X[:, xa + h * H:xa + (h + 1) * H], True, False)
+        wait("pe", e_pay, "one%d" % t)
+        e_idx = sig(pe.matmul(B[0][:, 0:W], T.ID[:], T.LV[:, N * t:N * t + N, N * r:N * r + C // 16], False, True))
+        wait("ve", e_law, e_idx)
+        e_iu = sig(ve.tensor_copy(T.IDX[:, W * t:W * t + W], B[0][:, 0:W]))
+        wait("ve", e_iu)
+        wait("ac", e_law, e_iu)
+        e_col = sig(ve.tensor_copy(T.COL[:, c0:c0 + H], T.LAW[:, 0:S * S].indirect(T.IDX[:, W * t:W * t + W // 2])))
+        sig(ac.activation(T.COL[:, c0 + H:c0 + M], T.LAW[:, 0:S * S].indirect(T.IDX[:, W * t + W // 2:W * t + W]), F.Copy), e_col)
+        wait("g", e_col)
+        for call in calls_two:
+            g.remote_dma_fused([RemoteDMATransfer(dst_ids=[dst_id(q)], dma_engine_mask=bits(e), remote_sem=T.sem["two%d" % t],
+                                                  src=T.COL[:, c0 + C * q:c0 + C * q + C],
+                                                  dst=T.LD[:, c0 + C * r:c0 + C * r + C]) for q, e in call],
+                               local_sem=T.sem.left)
+            total["left"] += sum(len(e) for q, e in call)
+        wait("pe", late["p1"], late["p2"], e_col)
+        e_first = new()
+        for h in range(2):
+            sig(pe.matmul(B[2 + h][:, 0:H], T.P1[:], T.COL[:, c0 + h * H:c0 + (h + 1) * H], False, True), e_first)
+        own = (C * r) // H
+        pe.matmul(B[4 + own][:, C * r - own * H:C * r - own * H + C], T.P2[:], T.COL[:, c0 + C * r:c0 + C * r + C], False, False)
+        ready = new()
+        p0 = 2 * W * t
+        if t < R - 1:
+            f0 = 2 * M * t
+            wait("ve", last_scatter[0])
+            wait("ac", last_scatter[0])
+            e_gp = sig(ve.tensor_copy(T.PF[:, f0:f0 + M], T.TB[:, 0:P].indirect(T.U0[:, (t + 1) * W:(t + 2) * W])))
+            sig(ac.activation(T.PF[:, f0 + M:f0 + 2 * M],
+                              T.TB[:, 0:P].indirect(T.U0[:, (R + t + 1) * W:(R + t + 2) * W]), F.Copy), e_gp)
+            wait("pe", e_ef, e_gp)
+            e_pw = sig(wrap(B[6][:, 0:2 * W], T.EF, T.PF, f0, f0 + 2 * M, True, True))
+            last_scatter[0] = e_gp
+            scatter(t + 1, 0, 0, EARLY)
+            wait("ve", e_pw)
+            e = sig(ve.tensor_tensor(T.PI[:, p0:p0 + W], B[6][:, 0:W], T.LA[:, (t + 1) * W:(t + 2) * W], A.max))
+            sig(ve.tensor_tensor(T.PI[:, p0 + W:p0 + 2 * W], B[6][:, W:2 * W], T.LB[:, (t + 1) * W:(t + 2) * W], A.max), e)
+            p1 = p0 + 2 * W
+        else:
+            wait("pe", last_scatter[0])
+            e_pw = sig(wrap(B[6][:, 0:P // 16], T.EF, T.TB, 0, P, True, True))
+            wait("ve", late["iw"], e_pw)
+            p1 = p0 + P // 16
+            e = sig(ve.tensor_tensor(T.PI[:, p0:p1], B[6][:, 0:P // 16], T.IW[:], A.max))
+        wait("ve", e)
+        sig(ve.tensor_copy(T.UP[:, p0:p1], T.PI[:, p0:p1]), ready)
+        wait("ac", e_first)
+        for h in range(2):
+            sig(ac.activation(T.V[:, v0 + h * H:v0 + (h + 1) * H], B[2 + h][:, 0:H], F.Copy), ready)
+        wait("pe", "two%d" % t)
+        e_second = []
+        for h in range(2):
+            runs = [(h * H, (h + 1) * H)]
+            if h == own:
+                runs = [(a, b) for a, b in [(h * H, C * r), (C * r + C, (h + 1) * H)] if a < b]
+            for i, (a, b) in enumerate(runs):
+                ins = pe.matmul(B[4 + h][:, a - h * H:b - h * H], T.P2[:], T.LD[:, c0 + a:c0 + b], False, i == len(runs) - 1)
+            e_second.append(sig(ins))
+        wait("ve", e_second[0])
+        sig(ve.tensor_copy(T.V[:, v0 + M:v0 + M + H], B[4][:, 0:H]), ready)
+        wait("ac", e_second[1])
+        sig(ac.activation(T.V[:, v0 + M + H:v0 + 2 * M], B[5][:, 0:H], F.Copy), ready)
+
+    wait("ve", ready)
+    wait("ac", ready)
+    p0 = 2 * W * (R - 1)
+    made = []
+    for i, (a, b) in enumerate(CHUNKS):
+        src = T.V[:, 0:P + R * 2 * M].indirect(T.UP[:, p0 + a // 16:p0 + b // 16])
+        made.append(sig(ve.tensor_copy(T.Y[:, a:b], src) if i % 2 == 0 else ac.activation(T.Y[:, a:b], src, F.Copy)))
+    e_out = new()
+    for i, (a, b) in enumerate(CHUNKS):
+        q = "ac" if i == len(CHUNKS) - 1 else "sy"
+        wait(q, made[i])
+        sig(queue[q].dma_start(T.y[:, a:b], T.Y[:, a:b]), e_out, 16)
+    wait("g", "left")
+    wait("g", *[ev for ev in total if ev not in seen and ev != e_out])
+    wait("sy", e_out)

@@ -1,14 +1,16 @@
 from concourse.bass import DstId, RemoteDMATransfer
-from concourse.mybir import AluOpType, ActivationFunctionType
+from concourse.mybir import AluOpType, AxisListType, ActivationFunctionType
 
 N, P, S, C, R = 6, 2048, 80, 96, 3
 M = N * C
 W = M // 16
 H = M // 2
-SLOT = 40
-EARLY = 480
+PIECE = C // 8
+SLOT = 16
+CUTS = [(0, 1152), (384, 1152), (384, 1056)]
+HALF = 5 * 63
 LAW_A = 4480
-CHUNKS = [(0, 512), (512, 1024), (1024, 1536), (1536, 2048)]
+CHUNKS = [(0, 448), (448, 896), (896, 1472), (1472, 2048)]
 
 SCRATCH = {
     "V": ("sbuf", [128, P + R * 2 * M], "bfloat16"),
@@ -16,13 +18,19 @@ SCRATCH = {
     "LA": ("sbuf", [128, R * W], "int32"),
     "LB": ("sbuf", [128, R * W], "int32"),
     "U0": ("sbuf", [128, 2 * R * W], "uint16"),
-    "TB": ("sbuf", [128, P], "float32"),
-    "RAMP": ("sbuf", [128, M], "float32"),
+    "TB": ("sbuf", [128, P], "bfloat16"),
+    "RAMP": ("sbuf", [128, 320], "int32"),
+    "RA": ("sbuf", [128, 320], "int32"),
+    "RB": ("sbuf", [128, 320], "int32"),
+    "VALS": ("sbuf", [128, R * 2 * M], "bfloat16"),
+    "C0": ("sbuf", [128, 4], "float32"),
+    "MC": ("sbuf", [128, 4], "float32"),
+    "C5": ("sbuf", [128, 4], "float32"),
     "ONES": ("sbuf", [128, 144], "bfloat16"),
     "E1": ("sbuf", [128, 144], "bfloat16"),
     "E80": ("sbuf", [128, 144], "bfloat16"),
-    "EF": ("sbuf", [128, 144], "float32"),
-    "ID": ("sbuf", [128, 128], "bfloat16"),
+    "EF": ("sbuf", [128, 144], "bfloat16"),
+    "IDW": ("sbuf", [128, 136], "bfloat16"),
     "PM": ("sbuf", [128, 128], "bfloat16"),
     "P1": ("sbuf", [128, 128], "bfloat16"),
     "P2": ("sbuf", [128, 128], "bfloat16"),
@@ -32,18 +40,19 @@ SCRATCH = {
     "IW0": ("sbuf", [128, 128], "float32"),
     "IW": ("sbuf", [128, 128], "float32"),
     "X": ("sbuf", [128, R * 2 * M], "bfloat16"),
+    "PAY": ("sbuf", [128, R * N * PIECE], "bfloat16"),
     "LV": ("sbuf", [128, R * N, SLOT], "bfloat16"),
     "IDX": ("sbuf", [128, R * W + 4], "uint16"),
     "COL": ("sbuf", [128, R * M], "bfloat16"),
     "LD": ("sbuf", [128, R * M], "bfloat16"),
-    "PF": ("sbuf", [128, (R - 1) * 2 * M], "float32"),
+    "PF": ("sbuf", [128, (R - 1) * 2 * M], "bfloat16"),
     "PI": ("sbuf", [128, (R - 1) * 2 * W + P // 16], "float32"),
     "UP": ("sbuf", [128, (R - 1) * 2 * W + P // 16], "uint16"),
     "Y": ("sbuf", [128, P], "float32"),
 }
 for _b in range(7):
     SCRATCH["B%d" % _b] = ("psum", [128, 512], "float32")
-SEMAPHORES = ["left"] + ["one%d" % t for t in range(R)] + ["two%d" % t for t in range(R)] + ["s%d" % k for k in range(110)]
+SEMAPHORES = ["left"] + ["one%d" % t for t in range(R)] + ["two%d" % t for t in range(R)] + ["s%d" % k for k in range(130)]
 
 
 def shared_engines(topo, src, dsts):
@@ -58,7 +67,7 @@ def bits(eng):
     return sum(1 << e for e in eng)
 
 
-def step_two_calls(topo, cores, r):
+def step_calls(topo, cores, r):
     def far(q):
         a, b = topo.chip(cores[r]), topo.chip(cores[q])
         return 0 if a == b else 1 if topo.mates(a, b) else 2 if topo.same_plane(a, b) else 3
@@ -67,6 +76,16 @@ def step_two_calls(topo, cores, r):
     first = others[:-1]
     each = len(eng) // len(first)
     return [[(q, eng[i * each:(i + 1) * each]) for i, q in enumerate(first)], [(others[-1], eng)]]
+
+
+def joined(ranks):
+    runs = []
+    for q in sorted(ranks):
+        if runs and runs[-1][1] == q:
+            runs[-1][1] = q + 1
+        else:
+            runs.append([q, q + 1])
+    return runs
 
 
 def rank_program(g, core, T, topo):
@@ -103,17 +122,22 @@ def rank_program(g, core, T, topo):
         return DstId(rid=rid, pnc=pid)
 
     others = [q for q in range(N) if q != r]
-    eng_one = shared_engines(topo, core, [cores[q] for q in others])
-    calls_two = step_two_calls(topo, cores, r)
+    calls = step_calls(topo, cores, r)
     total["left"] = 0
     for t in range(R):
-        total["one%d" % t] = sum(len(shared_engines(topo, cores[s], [cores[q] for q in range(N) if q != s])) for s in others)
-        total["two%d" % t] = sum(len(e) for s in others for call in step_two_calls(topo, cores, s) for q, e in call if q == r)
+        total["one%d" % t] = total["two%d" % t] = sum(
+            len(e) for s in others for call in step_calls(topo, cores, s) for q, e in call if q == r)
     B = [T["B%d" % b] for b in range(7)]
+    ident, shift8 = T.IDW[:, 8:136], T.IDW[:, 0:128]
 
-    def wrap(out, sel, src, lo, hi, start, stop):
-        for k in range(16):
-            ins = pe.matmul(out, sel[:, 16 - k:144 - k], src[:, lo + k:hi:16], start and k == 0, stop and k == 15)
+    def send(call, sem, src, dst):
+        g.remote_dma_fused([RemoteDMATransfer(dst_ids=[dst_id(q)], dma_engine_mask=bits(e), remote_sem=T.sem[sem],
+                                              src=src(q), dst=dst) for q, e in call], local_sem=T.sem.left)
+        total["left"] += sum(len(e) for q, e in call)
+
+    def wrap(out, sel, src, lo, hi, start, stop, n=16):
+        for k in range(n):
+            ins = pe.matmul(out, sel[:, 16 - k:144 - k], src[:, lo + k:hi:n], start and k == 0, stop and k == n - 1)
         return ins
 
     e_lb = sig(ac.dma_start(T.LB[:], T.lb[:]), n=16)
@@ -125,26 +149,43 @@ def rank_program(g, core, T, topo):
     e_tb = sig(ve.memset(T.TB[:], 0.0))
     wait("g", e_ones)
     e_e1 = sig(g.affine_select(T.E1[:], T.ONES[:], [[16, 9], [1001, 16]], A.is_equal, 0.0, -16, -1))
-    e_id = sig(g.affine_select(T.ID[:], T.ONES[:, 0:128], [[1, 128]], A.is_equal, 0.0, 0, -1))
-    e_ramp = sig(g.iota(T.RAMP[:], [[1, M]], 0, 0, allow_small_or_imprecise_dtypes=True))
+    e_ramp = sig(g.iota(T.RAMP[:, 0:HALF], [[256, 5], [1, 63]], 0, 0))
+    e_id = sig(g.affine_select(T.IDW[:], T.ONES[:, 0:136], [[1, 136]], A.is_equal, 0.0, -8, -1))
     e_pidx = sig(g.iota(T.PIDX[:, 0:1], [[1, 1]], 0, 1))
-    wait("g", e_id)
-    e_pm = sig(g.affine_select(T.PM[:], T.ID[:], [[0, 8], [1, 16]], A.not_equal, 0.0, 0, 0))
+    wait("g", e_e1, e_id)
+    e_pm = sig(g.affine_select(T.PM[:], ident, [[0, 8], [1, 16]], A.not_equal, 0.0, 0, 0))
     wait("ac", e_e1)
     e_e80 = sig(ac.activation(T.E80[:], T.E1[:], F.Copy, scale=float(S)))
-    e_ef = sig(ac.activation(T.EF[:], T.E1[:], F.Copy))
+    vals = {}
+    wait("ve", e_e1)
+    e = sig(ve.tensor_reduce(T.C0[:, 0:1], T.E1[:], AxisListType.X, A.add))
+    wait("ve", e)
+    e = sig(ve.tensor_scalar(T.MC[:, 0:1], T.C0[:, 0:1], 255.0, 1.0, A.mult, A.add))
+    e_c5 = sig(ve.tensor_scalar(T.C5[:, 0:1], T.C0[:, 0:1], -5.0, 5.0, A.mult, A.add))
+    wait("ve", e, e_ramp)
+    e = sig(ve.tensor_scalar(T.RA[:, 0:HALF], T.RAMP[:, 0:HALF], T.MC[:, 0:1], None, A.mult))
     wait("ve", e_lb)
     e_ub = sig(ve.tensor_copy(T.U0[:, R * W:2 * R * W], T.LB[:]))
+    wait("ve", e)
+    e_rb = sig(ve.tensor_scalar(T.RB[:, 0:HALF], T.RA[:, 0:HALF], 8, 255, A.logical_shift_right, A.bitwise_and))
     wait("ve", e_la)
     e_ua = sig(ve.tensor_copy(T.U0[:, 0:R * W], T.LA[:]))
 
     last_scatter = [e_tb]
 
-    def scatter(t, side, lo, hi):
-        c0 = side * R * W + t * W
-        wait("ve", last_scatter[0], e_ramp)
-        last_scatter[0] = sig(ve.tensor_scalar(T.TB[:, 0:P].indirect(T.U0[:, c0 + lo // 16:c0 + hi // 16]), T.RAMP[:, lo:hi],
-                                               1.0, float(P + 2 * M * t + side * M), A.mult, A.add))
+    def scatter(t, lo, hi):
+        for side in range(2):
+            a, b = max(lo - side * M, 0), min(hi - side * M, M)
+            if a < b:
+                c0 = side * R * W + t * W
+                i = 2 * t + side
+                wait("ve", vals[i], last_scatter[0])
+                last_scatter[0] = sig(ve.tensor_copy(T.TB[:, 0:P].indirect(T.U0[:, c0 + a // 16:c0 + b // 16]),
+                                                     T.VALS[:, i * M + a:i * M + b]))
+
+    def more_vals(i):
+        wait("ac", vals[0])
+        vals[i] = sig(ac.activation(T.VALS[:, i * M:(i + 1) * M], T.VALS[:, 0:M], F.Identity, bias=float(i * M // 64)))
 
     ready = None
     late = {}
@@ -161,36 +202,43 @@ def rank_program(g, core, T, topo):
             wait("ac", ready)
         e_xb = sig(ve.tensor_copy(T.X[:, xb:xb + H], win.indirect(off[:, ob:ob + W // 2])))
         sig(ac.activation(T.X[:, xb + H:xb + M], win.indirect(off[:, ob + W // 2:ob + W]), F.Copy), e_xb)
+        if t == 0:
+            wait("ve", e_rb)
+            e = sig(ve.tensor_scalar(T.VALS[:, 0:HALF], T.RB[:, 0:HALF], float(P // 64), None, A.add))
+            wait("ve", e, e_c5)
+            vals[0] = sig(ve.tensor_scalar(T.VALS[:, HALF:M], T.VALS[:, 0:M - HALF], T.C5[:, 0:1], None, A.add))
         wait("pe", e_e1, e_xb)
-        e_vw = sig(wrap(B[1][:, 0:W], T.E1, T.X, xb, xb + M, True, True))
+        y0 = N * PIECE * t
+        e_vw = sig(wrap(B[1][:, 0:N * PIECE], T.E1, T.X, xb, xb + M, True, True, 8))
         wait("ac", e_vw)
-        mine = T.LV[:, N * t + r, 0:W]
-        e_pay = sig(ac.activation(mine, B[1][:, 0:W], F.Copy))
+        e_pay = sig(ac.activation(T.PAY[:, y0:y0 + N * PIECE], B[1][:, 0:N * PIECE], F.Copy))
+        e_own = sig(ac.activation(T.LV[:, N * t + r, 0:PIECE], B[1][:, r * PIECE:(r + 1) * PIECE], F.Copy))
         wait("g", e_pay)
-        g.remote_dma_fused([RemoteDMATransfer(dst_ids=[dst_id(q) for q in others], dma_engine_mask=bits(eng_one),
-                                              remote_sem=T.sem["one%d" % t], srcs=[mine], dsts=[mine for q in others])],
-                           local_sem=T.sem.left)
-        total["left"] += len(eng_one)
+        for call in calls:
+            send(call, "one%d" % t, lambda q: T.PAY[:, y0 + PIECE * q:y0 + PIECE * (q + 1)], T.LV[:, N * t + r, 0:PIECE])
         if t == 0:
             wait("sy", e_pay)
             sig(sy.dma_start(T.LAW[:, LAW_A:S * S], T.law[:, LAW_A:S * S]), e_law, 16)
-            late["p1"] = sig(g.affine_select(T.P1[:], T.ID[:], [[0, 8], [1, 16]], A.not_equal, 0.0, -1, 0))
-            e = sig(g.affine_select(T.P2[:], T.ID[:], [[1, 128]], A.not_equal, -1.0, 0, -1))
+            late["p1"] = sig(g.affine_select(T.P1[:], ident, [[0, 8], [1, 16]], A.not_equal, 0.0, -1, 0))
+            e = sig(g.affine_select(T.P2[:], ident, [[1, 128]], A.not_equal, -1.0, 0, -1))
+            e_ef = sig(g.affine_select(T.EF[:], T.E1[:], [[16, 9], [1001, 16]], A.not_equal, 63.0, -15, -1))
             wait("g", e)
             e = sig(g.affine_select(T.P2[:], T.P2[:], [[0, 8], [1, 16]], A.is_ge, 0.0, -2, 0))
             wait("g", e)
             late["p2"] = sig(g.affine_select(T.P2[:], T.P2[:], [[16, 8], [1001, 16]], A.not_equal, 1.0, 1, -1))
-            late["iw0"] = sig(g.iota(T.IW0[:], [[16, 128]], 0, 1, allow_small_or_imprecise_dtypes=True))
             wait("ve", e_ua)
             wait("ac", e_ua)
-        scatter(t, 0, EARLY if t else 0, M)
-        scatter(t, 1, 0, M)
+        if t == 1:
+            late["iw0"] = sig(g.iota(T.IW0[:], [[16, 128]], 0, 1, allow_small_or_imprecise_dtypes=True))
+        e_xa = sig(ac.activation(T.X[:, xa:xa + M], win.indirect(off[:, oa:oa + W]), F.Copy))
+        for i in [[1, 2, 3], [4, 5], []][t]:
+            more_vals(i)
+        scatter(t, CUTS[t][0], CUTS[t][1])
         if t == 1:
             wait("ve", e_pidx)
             e = sig(ve.tensor_scalar(T.PA[:, 0:1], T.PIDX[:, 0:1], 128 - 16, None, A.bitwise_and))
             wait("ve", e)
             late["npa"] = sig(ve.tensor_scalar(T.NPA[:, 0:1], T.PA[:, 0:1], -1.0, None, A.mult))
-        e_xa = sig(ac.activation(T.X[:, xa:xa + M], win.indirect(off[:, oa:oa + W]), F.Copy))
         if t == 2:
             wait("ac", late["npa"], late["iw0"])
             late["iw"] = sig(ac.activation(T.IW[:], T.IW0[:], F.Identity, bias=T.NPA[:, 0:1]))
@@ -201,28 +249,38 @@ def rank_program(g, core, T, topo):
         wrap(B[0][:, 0:W], T.E80, T.X, xa, xa + M, True, False)
         for h in range(2):
             pe.matmul(B[2 + h][:, 0:H], T.PM[:], T.X[:, xa + h * H:xa + (h + 1) * H], True, False)
-        wait("pe", e_pay, "one%d" % t)
-        e_idx = sig(pe.matmul(B[0][:, 0:W], T.ID[:], T.LV[:, N * t:N * t + N, N * r:N * r + C // 16], False, True))
+        wait("pe", e_own, "one%d" % t)
+        pe.matmul(B[0][:, 0:W], ident, T.LV[:, N * t:N * t + N, 0:PIECE:2], False, False)
+        e_idx = sig(pe.matmul(B[0][:, 0:W], shift8, T.LV[:, N * t:N * t + N, 1:PIECE:2], False, True))
         wait("ve", e_law, e_idx)
         e_iu = sig(ve.tensor_copy(T.IDX[:, W * t:W * t + W], B[0][:, 0:W]))
         wait("ve", e_iu)
         wait("ac", e_law, e_iu)
-        e_col = sig(ve.tensor_copy(T.COL[:, c0:c0 + H], T.LAW[:, 0:S * S].indirect(T.IDX[:, W * t:W * t + W // 2])))
-        sig(ac.activation(T.COL[:, c0 + H:c0 + M], T.LAW[:, 0:S * S].indirect(T.IDX[:, W * t + W // 2:W * t + W]), F.Copy), e_col)
-        wait("g", e_col)
-        for call in calls_two:
-            g.remote_dma_fused([RemoteDMATransfer(dst_ids=[dst_id(q)], dma_engine_mask=bits(e), remote_sem=T.sem["two%d" % t],
-                                                  src=T.COL[:, c0 + C * q:c0 + C * q + C],
-                                                  dst=T.LD[:, c0 + C * r:c0 + C * r + C]) for q, e in call],
-                               local_sem=T.sem.left)
-            total["left"] += sum(len(e) for q, e in call)
-        wait("pe", late["p1"], late["p2"], e_col)
+
+        def columns(q, a, b, ev):
+            src = T.LAW[:, 0:S * S].indirect(T.IDX[:, W * t + a * C // 16:W * t + b * C // 16])
+            out = T.COL[:, c0 + a * C:c0 + b * C]
+            return sig(ve.tensor_copy(out, src) if q == "ve" else ac.activation(out, src, F.Copy), ev)
+        far = sorted(q for q, e in calls[0])
+        e_cols = [new(), new(), new()]
+        for a, b in joined(far[:len(far) // 2]):
+            columns("ve", a, b, e_cols[0])
+        for a, b in joined(far[len(far) // 2:]):
+            columns("ac", a, b, e_cols[0])
+        near = calls[1][0][0]
+        columns("ac", near, near + 1, e_cols[1])
+        columns("ve", r, r + 1, e_cols[2])
+        for i, call in enumerate(calls):
+            wait("g", e_cols[i])
+            send(call, "two%d" % t, lambda q: T.COL[:, c0 + C * q:c0 + C * q + C], T.LD[:, c0 + C * r:c0 + C * r + C])
+        wait("pe", late["p1"], late["p2"], e_ef, *e_cols)
         e_first = new()
         for h in range(2):
             sig(pe.matmul(B[2 + h][:, 0:H], T.P1[:], T.COL[:, c0 + h * H:c0 + (h + 1) * H], False, True), e_first)
         own = (C * r) // H
         pe.matmul(B[4 + own][:, C * r - own * H:C * r - own * H + C], T.P2[:], T.COL[:, c0 + C * r:c0 + C * r + C], False, False)
         ready = new()
+        scatter(t, CUTS[t][1], 2 * M)
         p0 = 2 * W * t
         if t < R - 1:
             f0 = 2 * M * t
@@ -231,10 +289,10 @@ def rank_program(g, core, T, topo):
             e_gp = sig(ve.tensor_copy(T.PF[:, f0:f0 + M], T.TB[:, 0:P].indirect(T.U0[:, (t + 1) * W:(t + 2) * W])))
             sig(ac.activation(T.PF[:, f0 + M:f0 + 2 * M],
                               T.TB[:, 0:P].indirect(T.U0[:, (R + t + 1) * W:(R + t + 2) * W]), F.Copy), e_gp)
-            wait("pe", e_ef, e_gp)
+            wait("pe", e_gp)
             e_pw = sig(wrap(B[6][:, 0:2 * W], T.EF, T.PF, f0, f0 + 2 * M, True, True))
             last_scatter[0] = e_gp
-            scatter(t + 1, 0, 0, EARLY)
+            scatter(t + 1, 0, CUTS[t + 1][0])
             wait("ve", e_pw)
             e = sig(ve.tensor_tensor(T.PI[:, p0:p0 + W], B[6][:, 0:W], T.LA[:, (t + 1) * W:(t + 2) * W], A.max))
             sig(ve.tensor_tensor(T.PI[:, p0 + W:p0 + 2 * W], B[6][:, W:2 * W], T.LB[:, (t + 1) * W:(t + 2) * W], A.max), e)

@@ -1,5 +1,5 @@
 from concourse.bass import DstId, RemoteDMATransfer
-from concourse.mybir import AluOpType, AxisListType, ActivationFunctionType
+from concourse.mybir import AluOpType, ActivationFunctionType
 
 N, P, S, C, R = 6, 2048, 80, 96, 3
 M = N * C
@@ -7,10 +7,69 @@ W = M // 16
 H = M // 2
 PIECE = C // 8
 SLOT = 16
-CUTS = [(0, 1152), (384, 1152), (384, 1056)]
-HALF = 5 * 63
+BASE = 63
+BLOCK = 8 * BASE
+UPTO = [[0, 1152, 1728], [1792, 2240, 2304], [3072, 3456, 3456]]
+LAST_AC = [[0, 512, 576], [576, 576, 576], [576, 576, 576]]
+FIRST_PIECE = 352
+TABLE_MM = [16, 20]
+VF_CUT = 576
+KW = 288
+LOOK = [None, (0, 1), (1, 2)]
+COOK = [("ac", "ve"), ("ve", "ac"), ("ac", "ve")]
+XA_VE = [0, 0, 2]
+RAW_VE = [1, 2, 2]
+HEAD_BY = ["ac", "ac", "ac"]
+PAY_BY = ["ac", "ve", "ac"]
+PLAN = [[0, 1], [2]]
+HEAD_SPLIT = True
+JOINT = False
+UH_BY = ["ac", "ac", "ac"]
+CONST_BY = "ac"
+COOK_FIRST = [False, False, False]
+OLD_EARLY = [2, 1, 1]
+XB_FIRST = [0, 3, 4]
+XB_SECOND = [0, 6, 6]
+XB_BY = ["ac", "ac", "ac"]
+OWN = ["ac", "ve", "ve"]
+PF_VE = [0, 576, 576]
+FIRSTS = [("ac", "ac"), ("ac", "ac"), ("ac", "ve")]
+RAMP = [(1, "ve"), (4, "ve"), (2, "ve"), (3, "ac")]
+SECOND_HALF = 4
 LAW_A = 4480
-CHUNKS = [(0, 448), (448, 896), (896, 1472), (1472, 2048)]
+CHUNKS = [(0, 128), (128, 416), (416, 640), (640, 1024), (1024, 1504), (1504, 2048)]
+
+UPTO = [[0, 1088, 1440], [1728, 2240, 3136], [3168, 3456, 3456]]
+LOOK = [None, (0, 2), (1, 2)]
+COOK = [("ve", "ac"), ("ve", "ac"), ("ve", "ac")]
+RAW_VE = [2, 3, 3]
+PAY_BY = ["ve", "ac", "ve"]
+COOK_FIRST = [False, False, False]
+OLD_EARLY = [2, 0, 0]
+XB_FIRST = [0, 6, 6]
+OWN = ["ac", "ve", "ve"]
+FIRSTS = [("ac", "ac"), ("ac", "ac"), ("ve", "ve")]
+LAST_AC = [[0, 512, 512], [512, 576, 576], [576, 576, 576]]
+VF_CUT = 512
+FIRST_PIECE = 128
+CHUNKS = [(0, 128), (128, 384), (384, 640), (640, 1024), (1024, 1536), (1536, 2048)]
+TABLE_MM = [16, 32]
+SECOND_HALF = -1
+JOINT = True
+HEAD_SPLIT = False
+LAW_A = 6400
+RAMP_PRE = 1
+RAMP = [(1, "ve"), (2, "ve"), (3, "ac"), (4, "ve")]
+RAW_VE = [3, 3, 3]
+PAY_BY = ["ac", "ac", "ve"]
+FIRST_PIECE = 0
+UPTO = [[0, 1024, 1440], [1472, 2176, 2304], [3136, 3456, 3456]]
+COOK = [("ve", "ac"), ("ac", "ve"), ("ac", "ve")]
+COOK_FIRST = [False, True, False]
+OWN = ["ac", "ac", "ve"]
+FIRSTS = [("ac", "ac"), ("ac", "ac"), ("ac", "ve")]
+LAST_AC = [[0, 512, 512], [512, 768, 768], [768, 768, 768]]
+CHUNKS = [(0, 128), (128, 384), (384, 672), (672, 1056), (1056, 1536), (1536, 2048)]
 
 SCRATCH = {
     "V": ("sbuf", [128, P + R * 2 * M], "bfloat16"),
@@ -18,41 +77,42 @@ SCRATCH = {
     "LA": ("sbuf", [128, R * W], "int32"),
     "LB": ("sbuf", [128, R * W], "int32"),
     "U0": ("sbuf", [128, 2 * R * W], "uint16"),
-    "TB": ("sbuf", [128, P], "bfloat16"),
-    "RAMP": ("sbuf", [128, 320], "int32"),
-    "RA": ("sbuf", [128, 320], "int32"),
-    "RB": ("sbuf", [128, 320], "int32"),
-    "VALS": ("sbuf", [128, R * 2 * M], "bfloat16"),
-    "C0": ("sbuf", [128, 4], "float32"),
-    "MC": ("sbuf", [128, 4], "float32"),
-    "C5": ("sbuf", [128, 4], "float32"),
-    "ONES": ("sbuf", [128, 144], "bfloat16"),
+    "TB": ("sbuf", [128, P + 2 * M], "bfloat16"),
+    "K": ("sbuf", [128, KW], "bfloat16"),
+    "TF": ("sbuf", [128, P], "float32"),
+    "VF": ("sbuf", [128, 2 * M], "float32"),
+    "WF": ("sbuf", [128, P // 16], "float32"),
+    "LT": ("sbuf", [128, 2 * W], "int32"),
+    "UT": ("sbuf", [128, 2 * W], "uint16"),
+    "IO": ("sbuf", [128, 64], "float32"),
+    "MK": ("sbuf", [128, 64], "float32"),
+    "PIDX": ("sbuf", [128, 4], "int32"),
+    "PA": ("sbuf", [128, 4], "int32"),
+    "ODD": ("sbuf", [128, 4], "float32"),
+    "ONES": ("sbuf", [128, KW], "bfloat16"),
     "E1": ("sbuf", [128, 144], "bfloat16"),
+    "I80": ("sbuf", [128, 136], "bfloat16"),
     "E80": ("sbuf", [128, 144], "bfloat16"),
+    "UH": ("sbuf", [128, R * N, PIECE], "bfloat16"),
     "EF": ("sbuf", [128, 144], "bfloat16"),
     "IDW": ("sbuf", [128, 136], "bfloat16"),
     "PM": ("sbuf", [128, 128], "bfloat16"),
+    "SW": ("sbuf", [128, 128], "bfloat16"),
     "P1": ("sbuf", [128, 128], "bfloat16"),
     "P2": ("sbuf", [128, 128], "bfloat16"),
-    "PIDX": ("sbuf", [128, 4], "int32"),
-    "PA": ("sbuf", [128, 4], "int32"),
-    "NPA": ("sbuf", [128, 4], "float32"),
-    "IW0": ("sbuf", [128, 128], "float32"),
-    "IW": ("sbuf", [128, 128], "float32"),
+    "XR": ("sbuf", [128, R * M], "bfloat16"),
     "X": ("sbuf", [128, R * 2 * M], "bfloat16"),
-    "PAY": ("sbuf", [128, R * N * PIECE], "bfloat16"),
-    "LV": ("sbuf", [128, R * N, SLOT], "bfloat16"),
+    "HEAD": ("sbuf", [128, R * 4, PIECE], "bfloat16"),
+    "PAY": ("sbuf", [128, R * N * N, SLOT], "bfloat16"),
     "IDX": ("sbuf", [128, R * W + 4], "uint16"),
     "COL": ("sbuf", [128, R * M], "bfloat16"),
-    "LD": ("sbuf", [128, R * M], "bfloat16"),
     "PF": ("sbuf", [128, (R - 1) * 2 * M], "bfloat16"),
-    "PI": ("sbuf", [128, (R - 1) * 2 * W + P // 16], "float32"),
     "UP": ("sbuf", [128, (R - 1) * 2 * W + P // 16], "uint16"),
     "Y": ("sbuf", [128, P], "float32"),
 }
-for _b in range(7):
+for _b in range(8):
     SCRATCH["B%d" % _b] = ("psum", [128, 512], "float32")
-SEMAPHORES = ["left"] + ["one%d" % t for t in range(R)] + ["two%d" % t for t in range(R)] + ["s%d" % k for k in range(130)]
+SEMAPHORES = ["left", "chain", "table"] + ["%s%d_%d" % (s, t, i) for s in ("one", "two") for t in range(R) for i in range(3)] + ["s%d" % k for k in range(129)]
 
 
 def shared_engines(topo, src, dsts):
@@ -73,9 +133,24 @@ def step_calls(topo, cores, r):
         return 0 if a == b else 1 if topo.mates(a, b) else 2 if topo.same_plane(a, b) else 3
     others = sorted([q for q in range(N) if q != r], key=lambda q: (-far(q), (q - r) % N))
     eng = shared_engines(topo, cores[r], [cores[q] for q in others])
-    first = others[:-1]
-    each = len(eng) // len(first)
-    return [[(q, eng[i * each:(i + 1) * each]) for i, q in enumerate(first)], [(others[-1], eng)]]
+    calls = []
+    for d in sorted({far(q) for q in others}, reverse=True):
+        these = sorted(q for q in others if far(q) == d)
+        each = len(eng) // len(these)
+        calls.append([(q, eng[i * each:(i + 1) * each]) for i, q in enumerate(these)])
+    return merged(calls, PLAN)
+
+
+def merged(calls, plan):
+    out = []
+    for these in plan:
+        ranks = [q for i in these for q, e in calls[i]]
+        eng = [x for q, e in calls[these[0]] for x in e]
+        share = [1] * len(ranks)
+        while sum(share) + min(share) <= len(eng):
+            share[share.index(min(share))] *= 2
+        out.append([(q, eng[sum(share[:i]):sum(share[:i + 1])]) for i, q in enumerate(ranks)])
+    return out
 
 
 def joined(ranks):
@@ -96,10 +171,11 @@ def rank_program(g, core, T, topo):
     A, F = AluOpType, ActivationFunctionType
     ve, ac, pe, sy = g.vector, g.scalar, g.tensor, g.sync
     queue = {"g": g, "ve": ve, "ac": ac, "pe": pe, "sy": sy}
-    total, seen, count = {}, {}, [0]
+    total, seen, count = {"chain": 0, "table": 0}, {}, [0]
 
     def new():
         name = "s%d" % count[0]
+        assert name in SEMAPHORES
         count[0] += 1
         total[name] = 0
         return name
@@ -111,28 +187,39 @@ def rank_program(g, core, T, topo):
         total[ev] += n
         return ev
 
+    def link(ins, chain="chain"):
+        total[chain] += 1
+        ins.then_inc(T.sem[chain], 1)
+        return (chain, total[chain])
+
     def wait(q, *evs):
         for ev in evs:
             if q not in seen.setdefault(ev, []):
                 seen[ev].append(q)
-                queue[q].wait_ge(T.sem[ev], total[ev])
+                name, n = ev if isinstance(ev, tuple) else (ev, total[ev])
+                if n:
+                    queue[q].wait_ge(T.sem[name], n)
 
     def dst_id(q):
         rid, pid, _ = topo.addr(cores[q])
         return DstId(rid=rid, pnc=pid)
 
+    def copy(q, out, src):
+        return ve.tensor_copy(out, src) if q == "ve" else ac.activation(out, src, F.Copy)
+
     others = [q for q in range(N) if q != r]
     calls = step_calls(topo, cores, r)
     total["left"] = 0
     for t in range(R):
-        total["one%d" % t] = total["two%d" % t] = sum(
-            len(e) for s in others for call in step_calls(topo, cores, s) for q, e in call if q == r)
-    B = [T["B%d" % b] for b in range(7)]
+        for i in range(len(calls)):
+            total["one%d_%d" % (t, i)] = total["two%d_%d" % (t, i)] = sum(
+                len(e) for s in others for q, e in step_calls(topo, cores, s)[i] if q == r)
+    B = [T["B%d" % b] for b in range(8)]
     ident, shift8 = T.IDW[:, 8:136], T.IDW[:, 0:128]
 
     def send(call, sem, src, dst):
         g.remote_dma_fused([RemoteDMATransfer(dst_ids=[dst_id(q)], dma_engine_mask=bits(e), remote_sem=T.sem[sem],
-                                              src=src(q), dst=dst) for q, e in call], local_sem=T.sem.left)
+                                              src=src(q), dst=dst(q)) for q, e in call], local_sem=T.sem.left)
         total["left"] += sum(len(e) for q, e in call)
 
     def wrap(out, sel, src, lo, hi, start, stop, n=16):
@@ -140,200 +227,431 @@ def rank_program(g, core, T, topo):
             ins = pe.matmul(out, sel[:, 16 - k:144 - k], src[:, lo + k:hi:n], start and k == 0, stop and k == n - 1)
         return ins
 
-    e_lb = sig(ac.dma_start(T.LB[:], T.lb[:]), n=16)
-    e_la = sig(ac.dma_start(T.LA[:], T.la[:]), n=16)
-    e_fld = sig(sy.dma_start(T.V[:, 0:P], T.fld[:]), n=16)
-    e_law = sig(sy.dma_start(T.LAW[:, 0:LAW_A], T.law[:, 0:LAW_A]), n=16)
+    def load_law(a, b, ev):
+        for k in range(2):
+            ev = sig(sy.dma_start(T.LAW[k:128:2, a:b], T.law[1 - k:128:2, a:b]), ev, 16)
+        return ev
 
+    e_lb = sig(ac.dma_start(T.LB[:], T.lb[:]), n=16)
+    e_fld = sig(sy.dma_start(T.V[:, 0:P], T.fld[:]), n=16)
+    e_la = sig(ac.dma_start(T.LA[:], T.la[:]), n=16)
     e_ones = sig(ve.memset(T.ONES[:], 1.0))
-    e_tb = sig(ve.memset(T.TB[:], 0.0))
-    wait("g", e_ones)
-    e_e1 = sig(g.affine_select(T.E1[:], T.ONES[:], [[16, 9], [1001, 16]], A.is_equal, 0.0, -16, -1))
-    e_ramp = sig(g.iota(T.RAMP[:, 0:HALF], [[256, 5], [1, 63]], 0, 0))
-    e_id = sig(g.affine_select(T.IDW[:], T.ONES[:, 0:136], [[1, 136]], A.is_equal, 0.0, -8, -1))
+    e_zero = sig(ve.memset(T.WF[:], 0.0))
+    wait("sy", e_zero)
+    e_tf = sig(sy.dma_start(T.TF[0:128:16, :], T.WF[:]), n=16)
+    e_law = load_law(0, LAW_A, None)
+    late = {"vals": [], "ramp": []}
+
+    def last_columns(a, b):
+        ins = g.iota(T.VF[:, a:b], [[1, b - a]], P + 4 * M + a, 0, allow_small_or_imprecise_dtypes=True)
+        late["vals"].append((a, sig(ins)))
+
     e_pidx = sig(g.iota(T.PIDX[:, 0:1], [[1, 1]], 0, 1))
-    wait("g", e_e1, e_id)
-    e_pm = sig(g.affine_select(T.PM[:], ident, [[0, 8], [1, 16]], A.not_equal, 0.0, 0, 0))
-    wait("ac", e_e1)
-    e_e80 = sig(ac.activation(T.E80[:], T.E1[:], F.Copy, scale=float(S)))
-    vals = {}
-    wait("ve", e_e1)
-    e = sig(ve.tensor_reduce(T.C0[:, 0:1], T.E1[:], AxisListType.X, A.add))
+    e_io = sig(g.iota(T.IO[:], [[1, 64]], 0, 0, allow_small_or_imprecise_dtypes=True))
+    wait("g", e_ones)
+    e_e1 = sig(g.affine_select(T.E1[:], T.ONES[:, 0:144], [[16, 9], [1001, 16]], A.is_equal, 0.0, -16, -1))
+    e_id = sig(g.affine_select(T.IDW[:], T.ONES[:, 0:136], [[1, 136]], A.is_equal, 0.0, -8, -1))
+    last_columns(0, VF_CUT)
+    e_sw = sig(g.affine_select(T.SW[:], T.ONES[:, 0:128], [[-2, 64], [1, 2]], A.is_equal, 0.0, -1, 1))
+    wait("g", e_e1, e_sw)
+    e_p2 = sig(g.affine_select(T.P2[:], T.SW[:], [[-2, 64], [1, 2]], A.not_equal, -1.0, -1, 1))
+    if CONST_BY == "g":
+        wait("g", e_id)
+        if JOINT:
+            e_i80 = e_e80 = sig(g.affine_select(T.E80[:], T.E1[:], [[16, 9], [1001, 16]], A.not_equal, float(S), -16, -1))
+        else:
+            e_i80 = sig(g.affine_select(T.I80[:], T.IDW[:], [[1, 136]], A.not_equal, float(S), -8, -1))
+    wait("ac", e_ones)
+    e_plus = sig(ac.activation(T.K[:], T.ONES[:], F.Silu, scale=float(2 * M // 64)))
+
+    wait("ve", e_pidx)
+    e = link(ve.tensor_scalar(T.PA[:, 0:1], T.PIDX[:, 0:1], 1, None, A.bitwise_and))
     wait("ve", e)
-    e = sig(ve.tensor_scalar(T.MC[:, 0:1], T.C0[:, 0:1], 255.0, 1.0, A.mult, A.add))
-    e_c5 = sig(ve.tensor_scalar(T.C5[:, 0:1], T.C0[:, 0:1], -5.0, 5.0, A.mult, A.add))
-    wait("ve", e, e_ramp)
-    e = sig(ve.tensor_scalar(T.RA[:, 0:HALF], T.RAMP[:, 0:HALF], T.MC[:, 0:1], None, A.mult))
+    e = link(ve.tensor_copy(T.ODD[:, 0:1], T.PA[:, 0:1]))
+    wait("ve", e, e_io)
+    e = link(ve.tensor_scalar(T.MK[:], T.IO[:], T.ODD[:, 0:1], None, A.mult))
+    wait("ve", e)
+    e = link(ve.tensor_tensor(T.TB[:, 0:BASE], T.IO[:, 0:BASE], T.MK[:, 0:BASE], A.subtract))
+    for k in (1, 2, 4):
+        wait("ve", e)
+        e = (sig if k == 4 else link)(ve.tensor_scalar(T.TB[:, k * BASE:2 * k * BASE], T.TB[:, 0:k * BASE], T.MK[:, k:k + 1], None, A.add))
+    wait("ve", e)
+    wait("ac", e)
+    e_ramp = new()
+
+    def ramp(q, a, b, lo, ev=None):
+        out, src, add = T.TB[:, a:b], T.TB[:, lo:lo + b - a], T.MK[:, (a - lo) // BASE:(a - lo) // BASE + 1]
+        return sig(ve.tensor_scalar(out, src, add, None, A.add) if q == "ve" else ac.activation(out, src, F.Identity, bias=add), ev)
+
+    def ramp_end(i):
+        lo = -(-P // BASE) * BASE
+        a = 5 * BLOCK + i * (5 * BLOCK - lo)
+        wait("ac", e_ramp)
+        late["ramp"].append((a - P, ramp("ac", a, min(a + 5 * BLOCK - lo, P + 2 * M), lo)))
     wait("ve", e_lb)
     e_ub = sig(ve.tensor_copy(T.U0[:, R * W:2 * R * W], T.LB[:]))
-    wait("ve", e)
-    e_rb = sig(ve.tensor_scalar(T.RB[:, 0:HALF], T.RA[:, 0:HALF], 8, 255, A.logical_shift_right, A.bitwise_and))
-    wait("ve", e_la)
-    e_ua = sig(ve.tensor_copy(T.U0[:, 0:R * W], T.LA[:]))
+    for k, q in RAMP[:RAMP_PRE]:
+        ramp(q, k * BLOCK, (k + 1) * BLOCK, 0, e_ramp)
 
-    last_scatter = [e_tb]
+    last, done, looked = [e_ramp, e_tf], [0, 0], {}
 
-    def scatter(t, lo, hi):
-        for side in range(2):
-            a, b = max(lo - side * M, 0), min(hi - side * M, M)
-            if a < b:
-                c0 = side * R * W + t * W
-                i = 2 * t + side
-                wait("ve", vals[i], last_scatter[0])
-                last_scatter[0] = sig(ve.tensor_copy(T.TB[:, 0:P].indirect(T.U0[:, c0 + a // 16:c0 + b // 16]),
-                                                     T.VALS[:, i * M + a:i * M + b]))
+    def scatter(upto):
+        while done[0] < min(upto, 4 * M):
+            i, a = divmod(done[0], M)
+            t, side = divmod(i, 2)
+            b = min(upto - i * M, M, a + (KW if t else M))
+            c0 = (side * R + t) * W
+            out, src = T.TB[:, 0:P].indirect(T.U0[:, c0 + a // 16:c0 + b // 16]), T.TB[:, P + side * M + a:P + side * M + b]
+            wait("ve", e_ua, e_ub, last[0], *[ev for lo, ev in late["ramp"] if lo < side * M + b])
+            assert side * M + b <= 5 * BLOCK - P + len(late["ramp"]) * (5 * BLOCK + P // -BASE * BASE)
+            if t == 0:
+                last[0] = link(ve.tensor_copy(out, src), "table")
+            else:
+                wait("ve", e_plus)
+                last[0] = link(ve.tensor_tensor(out, src, T.K[:, 0:b - a], A.add), "table")
+            done[0] = i * M + b
+        scatter_last("ve", upto - 4 * M)
 
-    def more_vals(i):
-        wait("ac", vals[0])
-        vals[i] = sig(ac.activation(T.VALS[:, i * M:(i + 1) * M], T.VALS[:, 0:M], F.Identity, bias=float(i * M // 64)))
+    def scatter_last(q, upto):
+        a = done[1]
+        if a < upto:
+            wait(q, last[1], late["turned"], *[ev for lo, ev in late["vals"] if lo < upto])
+            out, src = T.TF[:, 0:P].indirect(T.UT[:, a // 16:upto // 16]), T.VF[:, a:upto]
+            last[1] = sig(ve.tensor_copy(out, src) if q == "ve" else ac.activation(out, src, F.Silu))
+            done[1] = upto
 
+    def look_up(t):
+        scatter(2 * M * t)
+        ev = new()
+        for q, lo, hi in [("ve", 0, PF_VE[t]), ("ac", PF_VE[t], 2 * M)]:
+            for side in range(2):
+                a, b = max(lo - side * M, 0), min(hi - side * M, M)
+                if a < b:
+                    wait(q, last[0])
+                    f0, c0 = (2 * (t - 1) + side) * M, (side * R + t) * W
+                    sig(copy(q, T.PF[:, f0 + a:f0 + b], T.TB[:, 0:P].indirect(T.U0[:, c0 + a // 16:c0 + b // 16])), ev)
+        last[0] = looked[t] = ev
+
+    def slot(t, k):
+        scatter_last("ac", LAST_AC[t][k])
+        if t + 1 < R and LOOK[t + 1] == (t, k):
+            look_up(t + 1)
+        scatter(UPTO[t][k])
+
+    def wrap_pointers(t):
+        wait("pe", e_ef, looked[t])
+        return sig(wrap(B[6][:, 0:2 * W], T.EF, T.PF, 2 * M * (t - 1), 2 * M * t, True, True))
+
+    table, e_table = [0], []
+
+    def wrap_table(upto):
+        for i in range(table[0], upto):
+            h, k = divmod(i, 16)
+            ins = pe.matmul(B[6 + h][:, 0:P // 32], T.EF[:, 16 - k:144 - k], T.TB[:, h * P // 2 + k:(h + 1) * P // 2:16], k == 0, k == 15)
+            if k == 15:
+                e_table.append(sig(ins))
+        table[0] = max(table[0], upto)
+
+    own = (C * r) // H
     ready = None
-    late = {}
+    pairs = [sorted([q for q, e in call] + ([r] if len(call) == 1 else [])) for call in calls]
+    banks = [sorted(sum(pairs[:-1], [])), pairs[-1]]
+    heads = pairs[0] if HEAD_SPLIT else []
+    nh = len(heads)
+    rest = [s for s in range(N) if s not in heads]
+    order = heads + rest
+    slot0 = (N + 1) * r - rest.index(r)
+
+    def sums(a, b):
+        h = 0 if a in banks[0] else 1
+        i = banks[h].index(a)
+        return B[4 + h][:, C * i:C * (i + b - a)]
+
+    def seconds(t):
+        v1, evs = P + 2 * M * t + M, []
+        for i, call in enumerate(calls):
+            wait("pe", "two%d_%d" % (t, i))
+            runs = joined([q for q, e in call])
+            for a, b in runs:
+                ins = pe.matmul(sums(a, b), T.P2[:], T.V[:, v1 + a * C:v1 + b * C], False, i >= len(calls) - 2 and [a, b] == runs[-1])
+            if i >= len(calls) - 2:
+                evs.append(sig(ins))
+        return evs
+
+    def cooked(t, cook, by, ev, *after):
+        v1 = P + 2 * M * t + M
+        for h, q in enumerate(by):
+            wait(q, cook[h], *after)
+            for a, b in joined(banks[h]):
+                sig(copy(q, T.V[:, v1 + a * C:v1 + b * C], sums(a, b)), ev)
+        return ev
+
+    def half_wrap(out, src):
+        for k in range(8):
+            ins = pe.matmul(out, T.E1[:, 16 - k:144 - k], src(k), k == 0, k == 7)
+        return sig(ins)
+
     for t in range(R):
         win = T.V[:, 0:P + 2 * M * t]
-        xa, xb, c0, v0 = 2 * M * t, 2 * M * t + M, M * t, P + 2 * M * t
+        xa, xb, c0, v0, y0 = 2 * N * t, 2 * N * t + N, M * t, P + 2 * M * t, N * N * t
         if t == 0:
             off, oa, ob = T.U0, 0, R * W
-            wait("ve", e_ub, e_fld)
-            wait("ac", e_ub, e_fld)
+            gate = [e_ub, e_fld]
         else:
             off, oa, ob = T.UP, 2 * W * (t - 1), 2 * W * (t - 1) + W
-            wait("ve", ready)
-            wait("ac", ready)
-        e_xb = sig(ve.tensor_copy(T.X[:, xb:xb + H], win.indirect(off[:, ob:ob + W // 2])))
-        sig(ac.activation(T.X[:, xb + H:xb + M], win.indirect(off[:, ob + W // 2:ob + W]), F.Copy), e_xb)
-        if t == 0:
-            wait("ve", e_rb)
-            e = sig(ve.tensor_scalar(T.VALS[:, 0:HALF], T.RB[:, 0:HALF], float(P // 64), None, A.add))
-            wait("ve", e, e_c5)
-            vals[0] = sig(ve.tensor_scalar(T.VALS[:, HALF:M], T.VALS[:, 0:M - HALF], T.C5[:, 0:1], None, A.add))
-        wait("pe", e_e1, e_xb)
-        y0 = N * PIECE * t
-        e_vw = sig(wrap(B[1][:, 0:N * PIECE], T.E1, T.X, xb, xb + M, True, True, 8))
-        wait("ac", e_vw)
-        e_pay = sig(ac.activation(T.PAY[:, y0:y0 + N * PIECE], B[1][:, 0:N * PIECE], F.Copy))
-        e_own = sig(ac.activation(T.LV[:, N * t + r, 0:PIECE], B[1][:, r * PIECE:(r + 1) * PIECE], F.Copy))
-        wait("g", e_pay)
-        for call in calls:
-            send(call, "one%d" % t, lambda q: T.PAY[:, y0 + PIECE * q:y0 + PIECE * (q + 1)], T.LV[:, N * t + r, 0:PIECE])
-        if t == 0:
-            wait("sy", e_pay)
-            sig(sy.dma_start(T.LAW[:, LAW_A:S * S], T.law[:, LAW_A:S * S]), e_law, 16)
-            late["p1"] = sig(g.affine_select(T.P1[:], ident, [[0, 8], [1, 16]], A.not_equal, 0.0, -1, 0))
-            e = sig(g.affine_select(T.P2[:], ident, [[1, 128]], A.not_equal, -1.0, 0, -1))
-            e_ef = sig(g.affine_select(T.EF[:], T.E1[:], [[16, 9], [1001, 16]], A.not_equal, 63.0, -15, -1))
-            wait("g", e)
-            e = sig(g.affine_select(T.P2[:], T.P2[:], [[0, 8], [1, 16]], A.is_ge, 0.0, -2, 0))
-            wait("g", e)
-            late["p2"] = sig(g.affine_select(T.P2[:], T.P2[:], [[16, 8], [1001, 16]], A.not_equal, 1.0, 1, -1))
-            wait("ve", e_ua)
-            wait("ac", e_ua)
-        if t == 1:
-            late["iw0"] = sig(g.iota(T.IW0[:], [[16, 128]], 0, 1, allow_small_or_imprecise_dtypes=True))
-        e_xa = sig(ac.activation(T.X[:, xa:xa + M], win.indirect(off[:, oa:oa + W]), F.Copy))
-        for i in [[1, 2, 3], [4, 5], []][t]:
-            more_vals(i)
-        scatter(t, CUTS[t][0], CUTS[t][1])
-        if t == 1:
-            wait("ve", e_pidx)
-            e = sig(ve.tensor_scalar(T.PA[:, 0:1], T.PIDX[:, 0:1], 128 - 16, None, A.bitwise_and))
-            wait("ve", e)
-            late["npa"] = sig(ve.tensor_scalar(T.NPA[:, 0:1], T.PA[:, 0:1], -1.0, None, A.mult))
-        if t == 2:
-            wait("ac", late["npa"], late["iw0"])
-            late["iw"] = sig(ac.activation(T.IW[:], T.IW0[:], F.Identity, bias=T.NPA[:, 0:1]))
-        wait("pe", e_pm, e_e80, e_id)
-        for h in range(2):
-            pe.matmul(B[4 + h][:, 0:H], T.PM[:], T.X[:, xb + h * H:xb + (h + 1) * H], True, False)
-        wait("pe", e_xa)
-        wrap(B[0][:, 0:W], T.E80, T.X, xa, xa + M, True, False)
-        for h in range(2):
-            pe.matmul(B[2 + h][:, 0:H], T.PM[:], T.X[:, xa + h * H:xa + (h + 1) * H], True, False)
-        wait("pe", e_own, "one%d" % t)
-        pe.matmul(B[0][:, 0:W], ident, T.LV[:, N * t:N * t + N, 0:PIECE:2], False, False)
-        e_idx = sig(pe.matmul(B[0][:, 0:W], shift8, T.LV[:, N * t:N * t + N, 1:PIECE:2], False, True))
-        wait("ve", e_law, e_idx)
-        e_iu = sig(ve.tensor_copy(T.IDX[:, W * t:W * t + W], B[0][:, 0:W]))
-        wait("ve", e_iu)
-        wait("ac", e_law, e_iu)
+            gate = [ready, e_own] + ["two%d_%d" % (t - 1, i) for i in range(len(calls))]
+            cook = seconds(t - 1)
 
-        def columns(q, a, b, ev):
-            src = T.LAW[:, 0:S * S].indirect(T.IDX[:, W * t + a * C // 16:W * t + b * C // 16])
-            out = T.COL[:, c0 + a * C:c0 + b * C]
-            return sig(ve.tensor_copy(out, src) if q == "ve" else ac.activation(out, src, F.Copy), ev)
-        far = sorted(q for q, e in calls[0])
-        e_cols = [new(), new(), new()]
-        for a, b in joined(far[:len(far) // 2]):
-            columns("ve", a, b, e_cols[0])
-        for a, b in joined(far[len(far) // 2:]):
-            columns("ac", a, b, e_cols[0])
-        near = calls[1][0][0]
-        columns("ac", near, near + 1, e_cols[1])
-        columns("ve", r, r + 1, e_cols[2])
+        def fields(q, out, x, o0, a, b, ev):
+            return sig(copy(q, out[:, (x + a) * C:(x + b) * C], win.indirect(off[:, o0 + a * C // 16:o0 + b * C // 16])), ev)
+        wait("ac", *gate)
+        wait("ve", *gate)
+        e_head, e_raw = new(), new()
+        for ev, ranks, cut in [(e_head, heads, nh // 2), (e_raw, rest, min(RAW_VE[t], len(rest)))]:
+            for q, these in [("ve", ranks[:cut]), ("ac", ranks[cut:])]:
+                for a, b in joined(these):
+                    fields(q, T.XR, N * t + order.index(a) - a, ob, a, b, ev)
+        e_raw0 = e_head
+        if t == 0:
+            wait("ve", e_la)
+            e_ua = sig(ve.tensor_copy(T.U0[:, 0:R * W], T.LA[:]))
+            for k, q in RAMP[RAMP_PRE:]:
+                ramp(q, k * BLOCK, (k + 1) * BLOCK, 0, e_ramp)
+        if not nh:
+            e_raw0 = e_raw
+        wait("pe", e_e1, e_raw0)
+        if nh:
+            e = half_wrap(B[1][:, 0:nh * PIECE], lambda k: T.XR[:, c0 + k:c0 + nh * C:8])
+        early_cook = t > 0 and COOK_FIRST[t]
+        if early_cook:
+            e_cooked = cooked(t - 1, cook, COOK[t], new(), e_raw, e_raw0)
+        if nh:
+            wait(HEAD_BY[t], e)
+            e_head = sig(copy(HEAD_BY[t], T.HEAD[:, 4 * t:4 * t + nh, :], B[1][:, 0:nh * PIECE]))
+        wait("pe", e_raw)
+        e_vw = half_wrap(B[0][:, 0:(N - nh) * PIECE], lambda k: T.XR[:, c0 + nh * C + k:c0 + M:8])
+        if t > 0 and not early_cook:
+            e_cooked = cooked(t - 1, cook, COOK[t], new(), e_raw, e_raw0)
+        def pay():
+            wait(PAY_BY[t], e_vw)
+            return sig(copy(PAY_BY[t], T.PAY[:, y0 + slot0:y0 + slot0 + N - nh, 0:PIECE], B[0][:, 0:(N - nh) * PIECE]))
+        if t == 0:
+            e_pay = pay()
+            ramp_end(0)
+            scatter(FIRST_PIECE)
+            e = new()
+            if CONST_BY != "g":
+                sig(ve.tensor_scalar(T.PA[:, 1:2], T.PIDX[:, 0:1], 15, None, A.bitwise_and), e)
+            for side, lists in enumerate([T.LA, T.LB]):
+                sig(ve.tensor_scalar(T.LT[:, side * W:(side + 1) * W], lists[:, (R - 1) * W:R * W], float(P + 1), None, A.mult), e)
+            wait("ve", e)
+            if CONST_BY != "g":
+                late["rows"] = sig(ve.tensor_scalar(T.ODD[:, 1:2], T.PA[:, 1:2], 1.0, None, A.min))
+            e = link(ve.tensor_scalar(T.LT[:], T.LT[:], 4, P - 1, A.logical_shift_right, A.bitwise_and))
+            wait("ve", e)
+            late["turned"] = sig(ve.tensor_copy(T.UT[:], T.LT[:]))
+        slot(t, 0)
+        if t > 0:
+            e_pay = pay()
+        if not nh:
+            e_head = e_pay
         for i, call in enumerate(calls):
-            wait("g", e_cols[i])
-            send(call, "two%d" % t, lambda q: T.COL[:, c0 + C * q:c0 + C * q + C], T.LD[:, c0 + C * r:c0 + C * r + C])
-        wait("pe", late["p1"], late["p2"], e_ef, *e_cols)
-        e_first = new()
-        for h in range(2):
-            sig(pe.matmul(B[2 + h][:, 0:H], T.P1[:], T.COL[:, c0 + h * H:c0 + (h + 1) * H], False, True), e_first)
-        own = (C * r) // H
-        pe.matmul(B[4 + own][:, C * r - own * H:C * r - own * H + C], T.P2[:], T.COL[:, c0 + C * r:c0 + C * r + C], False, False)
-        ready = new()
-        scatter(t, CUTS[t][1], 2 * M)
-        p0 = 2 * W * t
-        if t < R - 1:
-            f0 = 2 * M * t
-            wait("ve", last_scatter[0])
-            wait("ac", last_scatter[0])
-            e_gp = sig(ve.tensor_copy(T.PF[:, f0:f0 + M], T.TB[:, 0:P].indirect(T.U0[:, (t + 1) * W:(t + 2) * W])))
-            sig(ac.activation(T.PF[:, f0 + M:f0 + 2 * M],
-                              T.TB[:, 0:P].indirect(T.U0[:, (R + t + 1) * W:(R + t + 2) * W]), F.Copy), e_gp)
-            wait("pe", e_gp)
-            e_pw = sig(wrap(B[6][:, 0:2 * W], T.EF, T.PF, f0, f0 + 2 * M, True, True))
-            last_scatter[0] = e_gp
-            scatter(t + 1, 0, CUTS[t + 1][0])
-            wait("ve", e_pw)
-            e = sig(ve.tensor_tensor(T.PI[:, p0:p0 + W], B[6][:, 0:W], T.LA[:, (t + 1) * W:(t + 2) * W], A.max))
-            sig(ve.tensor_tensor(T.PI[:, p0 + W:p0 + 2 * W], B[6][:, W:2 * W], T.LB[:, (t + 1) * W:(t + 2) * W], A.max), e)
-            p1 = p0 + 2 * W
+            wait("g", e_pay if i else e_head)
+            send(call, "one%d_%d" % (t, i),
+                 lambda q: T.PAY[:, y0 + slot0 + rest.index(q), 0:PIECE] if q in rest else T.HEAD[:, 4 * t + pairs[0].index(q), :],
+                 lambda q: T.PAY[:, y0 + (N + 1) * r, 0:PIECE])
+        if t == 0:
+            if LAW_A < S * S:
+                wait("sy", e_pay)
+                load_law(LAW_A, S * S, e_law)
+            wait("g", e_p2)
+            if CONST_BY == "g":
+                e_pm = sig(g.affine_select(T.PM[:], ident, [[0, 8], [1, 16]], A.not_equal, 0.0, 0, 0))
+                e_p1 = sig(g.affine_select(T.P1[:], T.SW[:], [[0, 8], [1, 16]], A.not_equal, 0.0, -1, 0))
+            e = sig(g.affine_select(T.P2[:], T.P2[:], [[0, 8], [1, 16]], A.is_ge, 0.0, -2, 0))
+            e_ef = sig(g.affine_select(T.EF[:], T.E1[:], [[16, 9], [1001, 16]], A.not_equal, float(BASE), -15, -1))
+            wait("g", e)
+            e_p2 = sig(g.affine_select(T.P2[:], T.P2[:], [[16, 8], [1001, 16]], A.not_equal, 1.0, 0, -1))
+            wait("ac", e_ua)
         else:
-            wait("pe", last_scatter[0])
-            e_pw = sig(wrap(B[6][:, 0:P // 16], T.EF, T.TB, 0, P, True, True))
-            wait("ve", late["iw"], e_pw)
-            p1 = p0 + P // 16
-            e = sig(ve.tensor_tensor(T.PI[:, p0:p1], B[6][:, 0:P // 16], T.IW[:], A.max))
-        wait("ve", e)
-        sig(ve.tensor_copy(T.UP[:, p0:p1], T.PI[:, p0:p1]), ready)
-        wait("ac", e_first)
-        for h in range(2):
-            sig(ac.activation(T.V[:, v0 + h * H:v0 + (h + 1) * H], B[2 + h][:, 0:H], F.Copy), ready)
-        wait("pe", "two%d" % t)
-        e_second = []
+            wait("ac", e_cooked)
+        n = XA_VE[t]
+        e_xa = fields("ac", T.X, xa, oa, n, N, None)
+        if n:
+            wait("ve", e_cooked if t else e_ua)
+            fields("ve", T.X, xa, oa, 0, n, e_xa)
+        if t == R - 1:
+            wrap_table(TABLE_MM[0])
+        wait("pe", e_xa, e_pay)
+        if JOINT:
+            if t == 0 and CONST_BY != "g":
+                wait("ac", e_e1)
+                e_e80 = sig(ac.activation(T.E80[:], T.E1[:], F.Copy, scale=float(S)))
+            wait("pe", e_e80, e_head)
+            wrap(B[1][:, 0:W], T.E80, T.X, xa * C, xa * C + M, True, False)
+        else:
+            e_uw = half_wrap(B[0][:, 0:N * PIECE], lambda k: T.X[:, xa * C + k:xa * C + M:8])
+        if t == 0:
+            ramp_end(1)
+            def scaled(out, src, by):
+                if CONST_BY == "ac":
+                    return sig(ac.activation(out, src, F.Copy, scale=by))
+                return sig(ve.tensor_scalar(out, src, by, None, A.mult))
+            if CONST_BY != "g":
+                wait(CONST_BY, e_id, e_sw, late["rows"])
+                e_pm = scaled(T.PM[:], ident, T.ODD[:, 1:2])
+                e_i80 = e_pm if JOINT else scaled(T.I80[:], T.IDW[:], float(S))
+                e_p1 = scaled(T.P1[:], T.SW[:], T.ODD[:, 1:2])
+        e_xb, n = e_raw, XB_FIRST[t]
+        if t > 0:
+            e_xb = new()
+            if n:
+                fields("ac", T.X, xb, ob, 0, n, e_xb)
+        e_uh = e_pay
+        if not JOINT and UH_BY[t] == "ac":
+            wait("ac", e_uw)
+            e_uh = sig(copy("ac", T.UH[:, N * t:N * t + N, :], B[0][:, 0:N * PIECE]))
+        n2 = XB_SECOND[t]
+        if t > 0 and n < n2:
+            fields("ac", T.X, xb, ob, n, n2, e_xb)
+        slot(t, 1)
+        if not JOINT and UH_BY[t] == "ve":
+            wait("ve", e_uw)
+            e_uh = sig(copy("ve", T.UH[:, N * t:N * t + N, :], B[0][:, 0:N * PIECE]))
+
+        def old_firsts(hs):
+            for h in hs:
+                pe.matmul(B[2 + h][:, 0:H], T.PM[:], T.X[:, xa * C + h * H:xa * C + (h + 1) * H], True, False)
+
+        def old_seconds():
+            wait("pe", e_xb)
+            for h in range(2):
+                for i, (a, b) in enumerate(joined(banks[h]) if t else [(s, s + 1) for s in banks[h]]):
+                    src = T.X[:, (xb + a) * C:(xb + b) * C] if t else T.XR[:, order.index(a) * C:order.index(a) * C + C]
+                    pe.matmul(sums(a, b), T.PM[:], src, i == 0, False)
+        wait("pe", e_pm, e_id, e_i80)
+        old_firsts(range(OLD_EARLY[t]))
+        if t == 0:
+            old_seconds()
+        wait("pe", e_uh, e_head)
+        wait("ve", e_law)
+        wait("ac", e_law)
+        e_cols = []
+
+        i0 = W * t
+        for i, call in enumerate(calls):
+            these, bank, k6 = pairs[i], B[(1, 0, 7)[i]], C // 16
+            strides = [(these[0], these[1] + 1, these[1] - these[0])] if len(these) == 2 else [(a, b, 1) for a, b in joined(these)]
+
+            def add(sel, src, scale, k, first, last):
+                for a, b, step in strides:
+                    j, n3 = these.index(a), len(range(a, b, step))
+                    ins = pe.matmul(bank[:, k6 * j:k6 * (j + n3)], sel, src(scale * a, scale * (b - 1) + 1, scale * step, k),
+                                    first and j == 0, last and b == strides[-1][1])
+                return ins
+            u = lambda a, b, step, k: T.UH[:, N * t + a:N * t + b:step, k:PIECE:2]
+            v = lambda a, b, step, k: T.PAY[:, y0 + a:y0 + b:step, k:PIECE:2]
+            if not JOINT:
+                add(T.I80[:, 8:136], u, 1, 0, True, False)
+                add(T.I80[:, 0:128], u, 1, 1, False, False)
+                wait("pe", "one%d_%d" % (t, i))
+                add(ident, v, N + 1, 0, False, False)
+                e = sig(add(shift8, v, N + 1, 1, False, True))
+                wait("ve", e)
+                e = sig(ve.tensor_copy(T.IDX[:, i0:i0 + k6 * len(these)], bank[:, 0:k6 * len(these)]))
+            elif i == 0:
+                wait("pe", *["one%d_%d" % (t, j) for j in range(len(calls))])
+                pe.matmul(B[1][:, 0:W], ident, v(0, N * N, N + 1, 0), False, False)
+                e = sig(pe.matmul(B[1][:, 0:W], shift8, v(0, N * N, N + 1, 1), False, True))
+                wait("ve", e)
+                e = sig(ve.tensor_copy(T.IDX[:, i0:i0 + W], B[1][:, 0:W]))
+            ev = new()
+            half = len(these) // 2
+            shares = [("ac", [call[0][0]]), (OWN[t], [r])] if r in these else [("ve", these[:half]), ("ac", these[half:])]
+            for q, ranks in shares:
+                for a, b in joined(ranks):
+                    out = T.V[:, v0 + M + a * C:v0 + M + b * C] if a == r else T.COL[:, c0 + a * C:c0 + b * C]
+                    j = W * t + k6 * a if JOINT else i0 + k6 * these.index(a)
+                    wait(q, e)
+                    ins = copy(q, out, T.LAW[:, 0:S * S].indirect(T.IDX[:, j:j + k6 * (b - a)]))
+                    if a == r:
+                        e_own = sig(ins)
+                    else:
+                        sig(ins, ev)
+            i0 += k6 * len(these)
+            e_cols.append(ev)
+            wait("g", ev)
+            send(call, "two%d_%d" % (t, i), lambda q: T.COL[:, c0 + C * q:c0 + C * q + C],
+                 lambda q: T.V[:, v0 + M + C * r:v0 + M + C * r + C])
+        if t == 0:
+            last_columns(VF_CUT, 2 * M)
+        ready = new()
+        early = t + 1 in looked
+        if early:
+            e_pw = wrap_pointers(t + 1)
+        slot(t, 2)
+        if t == R - 1:
+            wait("sy", last[1])
+            e_wf = sig(sy.dma_start(T.WF[:], T.TF[0:128:16, :]), n=16)
+        xb_late = t > 0 and max(n, n2) < N
+        if xb_late:
+            wait(XB_BY[t], e_cooked)
+            fields(XB_BY[t], T.X, xb, ob, max(n, n2), N, e_xb)
+        mine = T.V[:, v0 + M + C * r:v0 + M + C * r + C]
+        old_firsts(range(OLD_EARLY[t], 2))
+        if t > 0 and not xb_late:
+            old_seconds()
+        wait("pe", e_p1, e_own, *e_cols)
+        pe.matmul(B[2 + own][:, C * r - own * H:C * r - own * H + C], T.P1[:], mine, False, False)
+        e_first = new()
         for h in range(2):
             runs = [(h * H, (h + 1) * H)]
             if h == own:
                 runs = [(a, b) for a, b in [(h * H, C * r), (C * r + C, (h + 1) * H)] if a < b]
             for i, (a, b) in enumerate(runs):
-                ins = pe.matmul(B[4 + h][:, a - h * H:b - h * H], T.P2[:], T.LD[:, c0 + a:c0 + b], False, i == len(runs) - 1)
-            e_second.append(sig(ins))
-        wait("ve", e_second[0])
-        sig(ve.tensor_copy(T.V[:, v0 + M:v0 + M + H], B[4][:, 0:H]), ready)
-        wait("ac", e_second[1])
-        sig(ac.activation(T.V[:, v0 + M + H:v0 + 2 * M], B[5][:, 0:H], F.Copy), ready)
+                ins = pe.matmul(B[2 + h][:, a - h * H:b - h * H], T.P1[:], T.COL[:, c0 + a:c0 + b], False, i == len(runs) - 1)
+            sig(ins, e_first)
+        p0 = 2 * W * t
+        if t < R - 1 and not early:
+            e_pw = wrap_pointers(t + 1)
+        if xb_late:
+            old_seconds()
+        wait("pe", e_p2)
+        pe.matmul(sums(r, r + 1), T.P2[:], mine, False, False)
+        if t < R - 1:
+            wait("ve", e_pw)
+            sig(ve.tensor_copy(T.UP[:, p0:p0 + 2 * W], B[6][:, 0:2 * W]), ready)
+        for h, q in enumerate(FIRSTS[t]):
+            wait(q, e_first)
+            sig(copy(q, T.V[:, v0 + h * H:v0 + (h + 1) * H], B[2 + h][:, 0:H]), ready)
 
-    wait("ve", ready)
-    wait("ac", ready)
-    p0 = 2 * W * (R - 1)
+    wrap_table(max(TABLE_MM[1], 16))
+    cook = seconds(R - 1)
+    wrap_table(32)
+    e_up = []
+
+    def pointers(h):
+        a, b = h * P // 32, (h + 1) * P // 32
+        wait("ve", e_table[h], e_wf)
+        e = link(ve.tensor_tensor(T.WF[:, a:b], T.WF[:, a:b], B[6 + h][:, 0:P // 32], A.max))
+        wait("ve", e)
+        e_up.append(sig(ve.tensor_scalar(T.UP[:, p0 + a:p0 + b], T.WF[:, a:b], 0.25, None, A.add)))
+    pointers(0)
+    if SECOND_HALF < 0:
+        pointers(1)
+    cooked(R - 1, cook, COOK[0], ready)
     made = []
     for i, (a, b) in enumerate(CHUNKS):
-        src = T.V[:, 0:P + R * 2 * M].indirect(T.UP[:, p0 + a // 16:p0 + b // 16])
-        made.append(sig(ve.tensor_copy(T.Y[:, a:b], src) if i % 2 == 0 else ac.activation(T.Y[:, a:b], src, F.Copy)))
+        q = "ve" if i % 2 == 0 else "ac"
+        if i == SECOND_HALF:
+            pointers(1)
+        wait(q, ready, e_up[(b - 1) * 2 // P])
+        made.append(sig(copy(q, T.Y[:, a:b], T.V[:, 0:P + R * 2 * M].indirect(T.UP[:, p0 + a // 16:p0 + b // 16]))))
     e_out = new()
     for i, (a, b) in enumerate(CHUNKS):
         q = "ac" if i == len(CHUNKS) - 1 else "sy"
         wait(q, made[i])
         sig(queue[q].dma_start(T.y[:, a:b], T.Y[:, a:b]), e_out, 16)
     wait("g", "left")
-    wait("g", *[ev for ev in total if ev not in seen and ev != e_out])
+    wait("g", *[ev for ev in total if ev not in seen and ev not in (e_out, "chain", "table")])
     wait("sy", e_out)

@@ -5,80 +5,25 @@ N, P, S, C, R = 6, 2048, 80, 96, 3
 M = N * C
 W = M // 16
 H = M // 2
+K6 = C // 16
 PIECE = C // 8
 SLOT = 16
 BASE = 63
 BLOCK = 8 * BASE
-UPTO = [[0, 1152, 1728], [1792, 2240, 2304], [3072, 3456, 3456]]
-LAST_AC = [[0, 512, 576], [576, 576, 576], [576, 576, 576]]
-FIRST_PIECE = 352
-TABLE_MM = [16, 20]
-VF_CUT = 576
-KW = 288
-LOOK = [None, (0, 1), (1, 2)]
-COOK = [("ac", "ve"), ("ve", "ac"), ("ac", "ve")]
-XA_VE = [0, 0, 2]
-RAW_VE = [1, 2, 2]
-HEAD_BY = ["ac", "ac", "ac"]
-PAY_BY = ["ac", "ve", "ac"]
-PLAN = [[0, 1], [2]]
-HEAD_SPLIT = True
-JOINT = False
-UH_BY = ["ac", "ac", "ac"]
-CONST_BY = "ac"
-COOK_FIRST = [False, False, False]
-OLD_EARLY = [2, 1, 1]
-XB_FIRST = [0, 3, 4]
-XB_SECOND = [0, 6, 6]
-XB_BY = ["ac", "ac", "ac"]
-OWN = ["ac", "ve", "ve"]
-PF_VE = [0, 576, 576]
-FIRSTS = [("ac", "ac"), ("ac", "ac"), ("ac", "ve")]
-RAMP = [(1, "ve"), (4, "ve"), (2, "ve"), (3, "ac")]
-SECOND_HALF = 4
-LAW_A = 4480
-CHUNKS = [(0, 128), (128, 416), (416, 640), (640, 1024), (1024, 1504), (1504, 2048)]
-
-UPTO = [[0, 1088, 1440], [1728, 2240, 3136], [3168, 3456, 3456]]
-LOOK = [None, (0, 2), (1, 2)]
-COOK = [("ve", "ac"), ("ve", "ac"), ("ve", "ac")]
-RAW_VE = [2, 3, 3]
-PAY_BY = ["ve", "ac", "ve"]
-COOK_FIRST = [False, False, False]
-OLD_EARLY = [2, 0, 0]
-XB_FIRST = [0, 6, 6]
-OWN = ["ac", "ve", "ve"]
-FIRSTS = [("ac", "ac"), ("ac", "ac"), ("ve", "ve")]
-LAST_AC = [[0, 512, 512], [512, 576, 576], [576, 576, 576]]
-VF_CUT = 512
-FIRST_PIECE = 128
-CHUNKS = [(0, 128), (128, 384), (384, 640), (640, 1024), (1024, 1536), (1536, 2048)]
-TABLE_MM = [16, 32]
-SECOND_HALF = -1
-JOINT = True
-HEAD_SPLIT = False
-LAW_A = 6400
-RAMP_PRE = 1
-RAMP = [(1, "ve"), (2, "ve"), (3, "ac"), (4, "ve")]
-RAW_VE = [3, 3, 3]
-PAY_BY = ["ac", "ac", "ve"]
-FIRST_PIECE = 0
-UPTO = [[0, 1024, 1440], [1472, 2176, 2304], [3136, 3456, 3456]]
-COOK = [("ve", "ac"), ("ac", "ve"), ("ac", "ve")]
-COOK_FIRST = [False, True, False]
-OWN = ["ac", "ac", "ve"]
-FIRSTS = [("ac", "ac"), ("ac", "ac"), ("ac", "ve")]
-LAST_AC = [[0, 512, 512], [512, 768, 768], [768, 768, 768]]
-CHUNKS = [(0, 128), (128, 384), (384, 672), (672, 1056), (1056, 1536), (1536, 2048)]
+PLANS = [[[0, 1], [2]], [[0, 1], [2]], [[0], [1], [2]]]
+FIRST_PIECE, BEFORE, AFTER, END = 256, [1056, 2240], [1152, 2304], [1440, 2304]
+BY_SCALAR = [608, 864, 1024]
+TF_VALUES = [0, 608, 896, 2 * M]
+CHUNKS = [0, 96, 352, 672, 1120, 1632, 2048]
 
 SCRATCH = {
     "V": ("sbuf", [128, P + R * 2 * M], "bfloat16"),
     "LAW": ("sbuf", [128, S * S], "bfloat16"),
-    "LA": ("sbuf", [128, R * W], "int32"),
-    "LB": ("sbuf", [128, R * W], "int32"),
+    "L": ("sbuf", [128, 2, R * W], "int32"),
     "U0": ("sbuf", [128, 2 * R * W], "uint16"),
     "TB": ("sbuf", [128, P + 2 * M], "bfloat16"),
-    "K": ("sbuf", [128, KW], "bfloat16"),
+    "TT": ("sbuf", [128, P], "bfloat16"),
+    "K": ("sbuf", [128, H], "bfloat16"),
     "TF": ("sbuf", [128, P], "float32"),
     "VF": ("sbuf", [128, 2 * M], "float32"),
     "WF": ("sbuf", [128, P // 16], "float32"),
@@ -89,20 +34,13 @@ SCRATCH = {
     "PIDX": ("sbuf", [128, 4], "int32"),
     "PA": ("sbuf", [128, 4], "int32"),
     "ODD": ("sbuf", [128, 4], "float32"),
-    "ONES": ("sbuf", [128, KW], "bfloat16"),
-    "E1": ("sbuf", [128, 144], "bfloat16"),
-    "I80": ("sbuf", [128, 136], "bfloat16"),
-    "E80": ("sbuf", [128, 144], "bfloat16"),
-    "UH": ("sbuf", [128, R * N, PIECE], "bfloat16"),
-    "EF": ("sbuf", [128, 144], "bfloat16"),
-    "IDW": ("sbuf", [128, 136], "bfloat16"),
-    "PM": ("sbuf", [128, 128], "bfloat16"),
-    "SW": ("sbuf", [128, 128], "bfloat16"),
-    "P1": ("sbuf", [128, 128], "bfloat16"),
-    "P2": ("sbuf", [128, 128], "bfloat16"),
+    "ONES": ("sbuf", [128, H], "bfloat16"),
     "XR": ("sbuf", [128, R * M], "bfloat16"),
+    "XQ": ("sbuf", [128, M], "bfloat16"),
+    "XT": ("sbuf", [128, M], "bfloat16"),
     "X": ("sbuf", [128, R * 2 * M], "bfloat16"),
-    "HEAD": ("sbuf", [128, R * 4, PIECE], "bfloat16"),
+    "HEAD": ("sbuf", [128, 2, PIECE], "bfloat16"),
+    "UH": ("sbuf", [128, N, PIECE], "bfloat16"),
     "PAY": ("sbuf", [128, R * N * N, SLOT], "bfloat16"),
     "IDX": ("sbuf", [128, R * W + 4], "uint16"),
     "COL": ("sbuf", [128, R * M], "bfloat16"),
@@ -110,9 +48,13 @@ SCRATCH = {
     "UP": ("sbuf", [128, (R - 1) * 2 * W + P // 16], "uint16"),
     "Y": ("sbuf", [128, P], "float32"),
 }
+for _names, _n in [("E1 E80 EF", 144), ("IDW I80", 136), ("PM SW P1 P2", 128), ("QL QH QL63 QH63", 160)]:
+    for _name in _names.split():
+        SCRATCH[_name] = ("sbuf", [128, _n], "bfloat16")
 for _b in range(8):
     SCRATCH["B%d" % _b] = ("psum", [128, 512], "float32")
-SEMAPHORES = ["left", "chain", "table"] + ["%s%d_%d" % (s, t, i) for s in ("one", "two") for t in range(R) for i in range(3)] + ["s%d" % k for k in range(129)]
+SEMAPHORES = (["left", "chain", "table"] + ["%s%d_%d" % (s, t, i) for s in ("one", "two") for t in range(R) for i in range(3)]
+              + ["s%d" % k for k in range(129)])
 
 
 def shared_engines(topo, src, dsts):
@@ -127,30 +69,19 @@ def bits(eng):
     return sum(1 << e for e in eng)
 
 
-def step_calls(topo, cores, r):
+def step_calls(topo, cores, r, plan):
     def far(q):
         a, b = topo.chip(cores[r]), topo.chip(cores[q])
         return 0 if a == b else 1 if topo.mates(a, b) else 2 if topo.same_plane(a, b) else 3
-    others = sorted([q for q in range(N) if q != r], key=lambda q: (-far(q), (q - r) % N))
+    others = [q for q in range(N) if q != r]
     eng = shared_engines(topo, cores[r], [cores[q] for q in others])
+    classes = [[q for q in others if far(q) == d] for d in sorted({far(q) for q in others}, reverse=True)]
     calls = []
-    for d in sorted({far(q) for q in others}, reverse=True):
-        these = sorted(q for q in others if far(q) == d)
-        each = len(eng) // len(these)
-        calls.append([(q, eng[i * each:(i + 1) * each]) for i, q in enumerate(these)])
-    return merged(calls, PLAN)
-
-
-def merged(calls, plan):
-    out = []
     for these in plan:
-        ranks = [q for i in these for q, e in calls[i]]
-        eng = [x for q, e in calls[these[0]] for x in e]
-        share = [1] * len(ranks)
-        while sum(share) + min(share) <= len(eng):
-            share[share.index(min(share))] *= 2
-        out.append([(q, eng[sum(share[:i]):sum(share[:i + 1])]) for i, q in enumerate(ranks)])
-    return out
+        ranks = [q for i in these for q in classes[i]]
+        each = len(eng) // len(ranks)
+        calls.append([(q, eng[i * each:(i + 1) * each]) for i, q in enumerate(ranks)])
+    return calls
 
 
 def joined(ranks):
@@ -171,11 +102,10 @@ def rank_program(g, core, T, topo):
     A, F = AluOpType, ActivationFunctionType
     ve, ac, pe, sy = g.vector, g.scalar, g.tensor, g.sync
     queue = {"g": g, "ve": ve, "ac": ac, "pe": pe, "sy": sy}
-    total, seen, count = {"chain": 0, "table": 0}, {}, [0]
+    total, seen, count = {"chain": 0, "table": 0, "left": 0}, {}, [0]
 
     def new():
         name = "s%d" % count[0]
-        assert name in SEMAPHORES
         count[0] += 1
         total[name] = 0
         return name
@@ -197,87 +127,81 @@ def rank_program(g, core, T, topo):
             if q not in seen.setdefault(ev, []):
                 seen[ev].append(q)
                 name, n = ev if isinstance(ev, tuple) else (ev, total[ev])
-                if n:
-                    queue[q].wait_ge(T.sem[name], n)
-
-    def dst_id(q):
-        rid, pid, _ = topo.addr(cores[q])
-        return DstId(rid=rid, pnc=pid)
+                queue[q].wait_ge(T.sem[name], n)
 
     def copy(q, out, src):
         return ve.tensor_copy(out, src) if q == "ve" else ac.activation(out, src, F.Copy)
 
-    others = [q for q in range(N) if q != r]
-    calls = step_calls(topo, cores, r)
-    total["left"] = 0
+    def send(call, sem, src, dst):
+        ids = {q: DstId(rid=topo.addr(cores[q])[0], pnc=topo.addr(cores[q])[1]) for q, e in call}
+        g.remote_dma_fused([RemoteDMATransfer(dst_ids=[ids[q]], dma_engine_mask=bits(e), remote_sem=T.sem[sem],
+                                              src=src(q), dst=dst) for q, e in call], local_sem=T.sem.left)
+        total["left"] += sum(len(e) for q, e in call)
+
+    calls_of = [step_calls(topo, cores, r, plan) for plan in PLANS]
     for t in range(R):
-        for i in range(len(calls)):
+        for i in range(len(PLANS[t])):
             total["one%d_%d" % (t, i)] = total["two%d_%d" % (t, i)] = sum(
-                len(e) for s in others for q, e in step_calls(topo, cores, s)[i] if q == r)
+                len(e) for s in range(N) if s != r for q, e in step_calls(topo, cores, s, PLANS[t])[i] if q == r)
+    near = calls_of[0][-1][0][0]
     B = [T["B%d" % b] for b in range(8)]
     ident, shift8 = T.IDW[:, 8:136], T.IDW[:, 0:128]
 
-    def send(call, sem, src, dst):
-        g.remote_dma_fused([RemoteDMATransfer(dst_ids=[dst_id(q)], dma_engine_mask=bits(e), remote_sem=T.sem[sem],
-                                              src=src(q), dst=dst(q)) for q, e in call], local_sem=T.sem.left)
-        total["left"] += sum(len(e) for q, e in call)
-
-    def wrap(out, sel, src, lo, hi, start, stop, n=16):
+    def wrap(out, sel, src, lo, hi, stop, n=16):
         for k in range(n):
-            ins = pe.matmul(out, sel[:, 16 - k:144 - k], src[:, lo + k:hi:n], start and k == 0, stop and k == n - 1)
+            ins = pe.matmul(out, sel[:, 16 - k:144 - k], src[:, lo + k:hi:n], k == 0, stop and k == n - 1)
         return ins
 
-    def load_law(a, b, ev):
-        for k in range(2):
-            ev = sig(sy.dma_start(T.LAW[k:128:2, a:b], T.law[1 - k:128:2, a:b]), ev, 16)
-        return ev
+    def unturn(out, rows, start):
+        todo = [(e, o, sel, src) for e in range(2) for o in range(2) for sel, src in rows(o)]
+        for i, (e, o, sel, src) in enumerate(todo):
+            lo = 16 + 16 * (e - o)
+            ins = pe.matmul(out(e), sel[e][:, lo:lo + 128], src, start and i == 0, i == len(todo) - 1)
+        return sig(ins)
 
-    e_lb = sig(ac.dma_start(T.LB[:], T.lb[:]), n=16)
+    def load_law(k, ev):
+        return sig(sy.dma_start(T.LAW[k:128:2, :], T.law[1 - k:128:2, :]), ev, 16)
+
+    values = []
+
+    def last_values(i):
+        a, b = TF_VALUES[i:i + 2]
+        values.append((a, sig(g.iota(T.VF[:, a:b], [[1, b - a]], P + 4 * M + a, 0, allow_small_or_imprecise_dtypes=True))))
+
+    e_lb = sig(ac.dma_start(T.L[:, 1, :], T.lb[:]), n=16)
     e_fld = sig(sy.dma_start(T.V[:, 0:P], T.fld[:]), n=16)
-    e_la = sig(ac.dma_start(T.LA[:], T.la[:]), n=16)
+    e_la = sig(sy.dma_start(T.L[:, 0, :], T.la[:]), n=16)
     e_ones = sig(ve.memset(T.ONES[:], 1.0))
-    e_zero = sig(ve.memset(T.WF[:], 0.0))
-    wait("sy", e_zero)
-    e_tf = sig(sy.dma_start(T.TF[0:128:16, :], T.WF[:]), n=16)
-    e_law = load_law(0, LAW_A, None)
-    late = {"vals": [], "ramp": []}
-
-    def last_columns(a, b):
-        ins = g.iota(T.VF[:, a:b], [[1, b - a]], P + 4 * M + a, 0, allow_small_or_imprecise_dtypes=True)
-        late["vals"].append((a, sig(ins)))
-
+    e_law = load_law(0, None)
     e_pidx = sig(g.iota(T.PIDX[:, 0:1], [[1, 1]], 0, 1))
     e_io = sig(g.iota(T.IO[:], [[1, 64]], 0, 0, allow_small_or_imprecise_dtypes=True))
     wait("g", e_ones)
     e_e1 = sig(g.affine_select(T.E1[:], T.ONES[:, 0:144], [[16, 9], [1001, 16]], A.is_equal, 0.0, -16, -1))
     e_id = sig(g.affine_select(T.IDW[:], T.ONES[:, 0:136], [[1, 136]], A.is_equal, 0.0, -8, -1))
-    last_columns(0, VF_CUT)
-    e_sw = sig(g.affine_select(T.SW[:], T.ONES[:, 0:128], [[-2, 64], [1, 2]], A.is_equal, 0.0, -1, 1))
-    wait("g", e_e1, e_sw)
+    last_values(0)
+    wait("g", sig(g.affine_select(T.SW[:], T.ONES[:, 0:128], [[-2, 64], [1, 2]], A.is_equal, 0.0, -1, 1)))
     e_p2 = sig(g.affine_select(T.P2[:], T.SW[:], [[-2, 64], [1, 2]], A.not_equal, -1.0, -1, 1))
-    if CONST_BY == "g":
-        wait("g", e_id)
-        if JOINT:
-            e_i80 = e_e80 = sig(g.affine_select(T.E80[:], T.E1[:], [[16, 9], [1001, 16]], A.not_equal, float(S), -16, -1))
-        else:
-            e_i80 = sig(g.affine_select(T.I80[:], T.IDW[:], [[1, 136]], A.not_equal, float(S), -8, -1))
     wait("ac", e_ones)
     e_plus = sig(ac.activation(T.K[:], T.ONES[:], F.Silu, scale=float(2 * M // 64)))
 
     wait("ve", e_pidx)
-    e = link(ve.tensor_scalar(T.PA[:, 0:1], T.PIDX[:, 0:1], 1, None, A.bitwise_and))
-    wait("ve", e)
-    e = link(ve.tensor_copy(T.ODD[:, 0:1], T.PA[:, 0:1]))
-    wait("ve", e, e_io)
-    e = link(ve.tensor_scalar(T.MK[:], T.IO[:], T.ODD[:, 0:1], None, A.mult))
-    wait("ve", e)
+    wait("ve", link(ve.tensor_scalar(T.PA[:, 0:1], T.PIDX[:, 0:1], 1, None, A.bitwise_and)))
+    wait("ve", link(ve.tensor_copy(T.ODD[:, 0:1], T.PA[:, 0:1])), e_io)
+    wait("ve", link(ve.tensor_scalar(T.MK[:], T.IO[:], T.ODD[:, 0:1], None, A.mult)))
     e = link(ve.tensor_tensor(T.TB[:, 0:BASE], T.IO[:, 0:BASE], T.MK[:, 0:BASE], A.subtract))
     for k in (1, 2, 4):
+        if k == 2:
+            wait("sy", sig(ve.memset(T.WF[:], 0.0)))
+            e_tf = sig(sy.dma_start(T.TF[0:128:16, :], T.WF[:]), n=16)
+            load_law(1, e_law)
+        if k == 4:
+            wait("ve", e_lb)
+            e_ub = sig(ve.tensor_copy(T.U0[:, R * W:2 * R * W], T.L[:, 1, :]))
         wait("ve", e)
         e = (sig if k == 4 else link)(ve.tensor_scalar(T.TB[:, k * BASE:2 * k * BASE], T.TB[:, 0:k * BASE], T.MK[:, k:k + 1], None, A.add))
     wait("ve", e)
     wait("ac", e)
-    e_ramp = new()
+    e_ramp, ends = new(), []
 
     def ramp(q, a, b, lo, ev=None):
         out, src, add = T.TB[:, a:b], T.TB[:, lo:lo + b - a], T.MK[:, (a - lo) // BASE:(a - lo) // BASE + 1]
@@ -287,319 +211,235 @@ def rank_program(g, core, T, topo):
         lo = -(-P // BASE) * BASE
         a = 5 * BLOCK + i * (5 * BLOCK - lo)
         wait("ac", e_ramp)
-        late["ramp"].append((a - P, ramp("ac", a, min(a + 5 * BLOCK - lo, P + 2 * M), lo)))
-    wait("ve", e_lb)
-    e_ub = sig(ve.tensor_copy(T.U0[:, R * W:2 * R * W], T.LB[:]))
-    for k, q in RAMP[:RAMP_PRE]:
-        ramp(q, k * BLOCK, (k + 1) * BLOCK, 0, e_ramp)
+        ends.append((a - P, ramp("ac", a, min(a + 5 * BLOCK - lo, P + 2 * M), lo)))
+    ramp("ve", BLOCK, 2 * BLOCK, 0, e_ramp)
 
-    last, done, looked = [e_ramp, e_tf], [0, 0], {}
+    last, done, ev_of = [e_ramp, e_tf], [0, 0], {}
 
     def scatter(upto):
-        while done[0] < min(upto, 4 * M):
+        while done[0] < upto:
             i, a = divmod(done[0], M)
             t, side = divmod(i, 2)
-            b = min(upto - i * M, M, a + (KW if t else M))
+            b = min(upto - i * M, M, a + (H if t else M))
             c0 = (side * R + t) * W
             out, src = T.TB[:, 0:P].indirect(T.U0[:, c0 + a // 16:c0 + b // 16]), T.TB[:, P + side * M + a:P + side * M + b]
-            wait("ve", e_ua, e_ub, last[0], *[ev for lo, ev in late["ramp"] if lo < side * M + b])
-            assert side * M + b <= 5 * BLOCK - P + len(late["ramp"]) * (5 * BLOCK + P // -BASE * BASE)
+            wait("ve", ev_of["ua"], e_ub, last[0], *[ev for lo, ev in ends if lo < side * M + b])
             if t == 0:
                 last[0] = link(ve.tensor_copy(out, src), "table")
             else:
                 wait("ve", e_plus)
                 last[0] = link(ve.tensor_tensor(out, src, T.K[:, 0:b - a], A.add), "table")
             done[0] = i * M + b
-        scatter_last("ve", upto - 4 * M)
 
     def scatter_last(q, upto):
         a = done[1]
-        if a < upto:
-            wait(q, last[1], late["turned"], *[ev for lo, ev in late["vals"] if lo < upto])
-            out, src = T.TF[:, 0:P].indirect(T.UT[:, a // 16:upto // 16]), T.VF[:, a:upto]
-            last[1] = sig(ve.tensor_copy(out, src) if q == "ve" else ac.activation(out, src, F.Silu))
-            done[1] = upto
+        wait(q, last[1], ev_of["ut"], *[ev for lo, ev in values if lo < upto])
+        out, src = T.TF[:, 0:P].indirect(T.UT[:, a // 16:upto // 16]), T.VF[:, a:upto]
+        last[1] = sig(ve.tensor_copy(out, src) if q == "ve" else ac.activation(out, src, F.Silu))
+        done[1] = upto
 
-    def look_up(t):
-        scatter(2 * M * t)
-        ev = new()
-        for q, lo, hi in [("ve", 0, PF_VE[t]), ("ac", PF_VE[t], 2 * M)]:
-            for side in range(2):
-                a, b = max(lo - side * M, 0), min(hi - side * M, M)
-                if a < b:
-                    wait(q, last[0])
-                    f0, c0 = (2 * (t - 1) + side) * M, (side * R + t) * W
-                    sig(copy(q, T.PF[:, f0 + a:f0 + b], T.TB[:, 0:P].indirect(T.U0[:, c0 + a // 16:c0 + b // 16])), ev)
-        last[0] = looked[t] = ev
+    far = [[q for q, e in call] for call in calls_of[-1]]
+    banks = [[(sorted(far[0] + far[1]), 4, "ac"), (sorted([near, r]), 5, "ve")]] * (R - 1)
+    banks.append([(sorted(far[0] + [r]), 4, "ac"), (far[1], 0, "ve"), ([near], 5, "ve")])
 
-    def slot(t, k):
-        scatter_last("ac", LAST_AC[t][k])
-        if t + 1 < R and LOOK[t + 1] == (t, k):
-            look_up(t + 1)
-        scatter(UPTO[t][k])
-
-    def wrap_pointers(t):
-        wait("pe", e_ef, looked[t])
-        return sig(wrap(B[6][:, 0:2 * W], T.EF, T.PF, 2 * M * (t - 1), 2 * M * t, True, True))
-
-    table, e_table = [0], []
-
-    def wrap_table(upto):
-        for i in range(table[0], upto):
-            h, k = divmod(i, 16)
-            ins = pe.matmul(B[6 + h][:, 0:P // 32], T.EF[:, 16 - k:144 - k], T.TB[:, h * P // 2 + k:(h + 1) * P // 2:16], k == 0, k == 15)
-            if k == 15:
-                e_table.append(sig(ins))
-        table[0] = max(table[0], upto)
-
-    own = (C * r) // H
-    ready = None
-    pairs = [sorted([q for q, e in call] + ([r] if len(call) == 1 else [])) for call in calls]
-    banks = [sorted(sum(pairs[:-1], [])), pairs[-1]]
-    heads = pairs[0] if HEAD_SPLIT else []
-    nh = len(heads)
-    rest = [s for s in range(N) if s not in heads]
-    order = heads + rest
-    slot0 = (N + 1) * r - rest.index(r)
-
-    def sums(a, b):
-        h = 0 if a in banks[0] else 1
-        i = banks[h].index(a)
-        return B[4 + h][:, C * i:C * (i + b - a)]
+    def sums(t, a, b):
+        ranks, bank, q = [x for x in banks[t] if a in x[0]][0]
+        return B[bank][:, C * ranks.index(a):C * (ranks.index(a) + b - a)]
 
     def seconds(t):
         v1, evs = P + 2 * M * t + M, []
-        for i, call in enumerate(calls):
+        for i, call in enumerate(calls_of[t]):
             wait("pe", "two%d_%d" % (t, i))
             runs = joined([q for q, e in call])
             for a, b in runs:
-                ins = pe.matmul(sums(a, b), T.P2[:], T.V[:, v1 + a * C:v1 + b * C], False, i >= len(calls) - 2 and [a, b] == runs[-1])
-            if i >= len(calls) - 2:
-                evs.append(sig(ins))
+                ins = pe.matmul(sums(t, a, b), T.P2[:], T.V[:, v1 + a * C:v1 + b * C], False, [a, b] == runs[-1])
+            evs.append(sig(ins))
         return evs
 
-    def cooked(t, cook, by, ev, *after):
+    def replace(t, evs, ev, *after):
         v1 = P + 2 * M * t + M
-        for h, q in enumerate(by):
-            wait(q, cook[h], *after)
-            for a, b in joined(banks[h]):
-                sig(copy(q, T.V[:, v1 + a * C:v1 + b * C], sums(a, b)), ev)
+        for (ranks, bank, q), e in zip(banks[t], evs):
+            wait(q, e, *after)
+            for a, b in joined(ranks):
+                sig(copy(q, T.V[:, v1 + a * C:v1 + b * C], sums(t, a, b)), ev)
         return ev
 
-    def half_wrap(out, src):
-        for k in range(8):
-            ins = pe.matmul(out, T.E1[:, 16 - k:144 - k], src(k), k == 0, k == 7)
-        return sig(ins)
+    def species(out, x, a, b, ev):
+        wait("ve", ev)
+        wait("ve", link(ve.transpose(T.XT[:, a:b], T.XR[:, x + a:x + b])))
+        return sig(ve.tensor_copy(out, T.XT[:, a:b:16]))
 
+    own = (C * r) // H
     for t in range(R):
+        end, calls = t == R - 1, calls_of[t]
         win = T.V[:, 0:P + 2 * M * t]
-        xa, xb, c0, v0, y0 = 2 * N * t, 2 * N * t + N, M * t, P + 2 * M * t, N * N * t
+        xa, xb, c0, v0, y0, p0 = 2 * N * t, 2 * N * t + N, M * t, P + 2 * M * t, N * N * t, 2 * W * t
+        groups = [sorted([q for q, e in call] + ([r] if len(call) == 1 else [])) for call in calls]
+        heads = groups[0] if end else []
+        rest = [s for s in range(N) if s not in heads]
+        order, slot0, pw = heads + rest, y0 + (N + 1) * r - rest.index(r), K6 if end else PIECE
         if t == 0:
-            off, oa, ob = T.U0, 0, R * W
-            gate = [e_ub, e_fld]
+            off, oa, ob, gate = T.U0, 0, R * W, [e_ub, e_fld]
         else:
-            off, oa, ob = T.UP, 2 * W * (t - 1), 2 * W * (t - 1) + W
-            gate = [ready, e_own] + ["two%d_%d" % (t - 1, i) for i in range(len(calls))]
-            cook = seconds(t - 1)
+            off, oa, ob = T.UP, p0 - 2 * W, p0 - W
+            gate = [ready, e_own] + ["two%d_%d" % (t - 1, i) for i in range(len(calls_of[t - 1]))]
+            e_sums = seconds(t - 1)
 
-        def fields(q, out, x, o0, a, b, ev):
-            return sig(copy(q, out[:, (x + a) * C:(x + b) * C], win.indirect(off[:, o0 + a * C // 16:o0 + b * C // 16])), ev)
+        def fields(q, out, x, o0, a, b, ev=None):
+            return sig(copy(q, out[:, (x + a) * C:(x + b) * C], win.indirect(off[:, o0 + a * K6:o0 + b * K6])), ev)
+
         wait("ac", *gate)
         wait("ve", *gate)
-        e_head, e_raw = new(), new()
-        for ev, ranks, cut in [(e_head, heads, nh // 2), (e_raw, rest, min(RAW_VE[t], len(rest)))]:
-            for q, these in [("ve", ranks[:cut]), ("ac", ranks[cut:])]:
-                for a, b in joined(these):
-                    fields(q, T.XR, N * t + order.index(a) - a, ob, a, b, ev)
-        e_raw0 = e_head
-        if t == 0:
-            wait("ve", e_la)
-            e_ua = sig(ve.tensor_copy(T.U0[:, 0:R * W], T.LA[:]))
-            for k, q in RAMP[RAMP_PRE:]:
-                ramp(q, k * BLOCK, (k + 1) * BLOCK, 0, e_ramp)
-        if not nh:
-            e_raw0 = e_raw
-        wait("pe", e_e1, e_raw0)
-        if nh:
-            e = half_wrap(B[1][:, 0:nh * PIECE], lambda k: T.XR[:, c0 + k:c0 + nh * C:8])
-        early_cook = t > 0 and COOK_FIRST[t]
-        if early_cook:
-            e_cooked = cooked(t - 1, cook, COOK[t], new(), e_raw, e_raw0)
-        if nh:
-            wait(HEAD_BY[t], e)
-            e_head = sig(copy(HEAD_BY[t], T.HEAD[:, 4 * t:4 * t + nh, :], B[1][:, 0:nh * PIECE]))
-        wait("pe", e_raw)
-        e_vw = half_wrap(B[0][:, 0:(N - nh) * PIECE], lambda k: T.XR[:, c0 + nh * C + k:c0 + M:8])
-        if t > 0 and not early_cook:
-            e_cooked = cooked(t - 1, cook, COOK[t], new(), e_raw, e_raw0)
-        def pay():
-            wait(PAY_BY[t], e_vw)
-            return sig(copy(PAY_BY[t], T.PAY[:, y0 + slot0:y0 + slot0 + N - nh, 0:PIECE], B[0][:, 0:(N - nh) * PIECE]))
-        if t == 0:
-            e_pay = pay()
-            ramp_end(0)
-            scatter(FIRST_PIECE)
-            e = new()
-            if CONST_BY != "g":
-                sig(ve.tensor_scalar(T.PA[:, 1:2], T.PIDX[:, 0:1], 15, None, A.bitwise_and), e)
-            for side, lists in enumerate([T.LA, T.LB]):
-                sig(ve.tensor_scalar(T.LT[:, side * W:(side + 1) * W], lists[:, (R - 1) * W:R * W], float(P + 1), None, A.mult), e)
+        if not end:
+            e_raw = fields("ve", T.XR, N * t, ob, 0, 2 + t)
+            fields("ac", T.XR, N * t, ob, 2 + t, N, e_raw)
+            if t == 0:
+                wait("ve", e_la)
+                ev_of["ua"] = sig(ve.tensor_copy(T.U0[:, 0:R * W], T.L[:, 0, :]))
+                e = sig(ve.tensor_scalar(T.LT[:], T.L[:, :, (R - 1) * W:R * W], float(P + 1), None, A.mult))
+                ramp("ve", 2 * BLOCK, 3 * BLOCK, 0, e_ramp)
+                ramp("ac", 4 * BLOCK, 5 * BLOCK, 0, e_ramp)
+                wait("ve", e)
+                e_lt = link(ve.tensor_scalar(T.LT[:], T.LT[:], 4, P - 1, A.logical_shift_right, A.bitwise_and))
+                ramp("ve", 3 * BLOCK, 4 * BLOCK, 0, e_ramp)
+            wait("pe", e_e1, e_raw)
+            e = sig(wrap(B[0][:, 0:N * PIECE], T.E1, T.XR, c0, c0 + M, True, 8))
+            if t > 0:
+                e_new = replace(t - 1, e_sums, new(), e_raw)
+            wait("ac", e)
+            e_head = e_pay = sig(copy("ac", T.PAY[:, slot0:slot0 + N, 0:pw], B[0][:, 0:N * PIECE]))
+            if t == 0:
+                ramp_end(0)
+                scatter(FIRST_PIECE)
+                wait("ve", e_lt)
+                ev_of["ut"] = sig(ve.tensor_copy(T.UT[:], T.LT[:]))
+        else:
+            e_first_call, e_rest = new(), new()
+            for q, s in zip(["ve", "ac"], heads):
+                fields(q, T.XR, N * t + order.index(s) - s, ob, s, s + 1, e_first_call)
+            e_head = species(T.HEAD[:, :, 0:pw], c0, 0, 2 * C, e_first_call)
+            for a, b in joined(rest):
+                fields("ac", T.XR, N * t + order.index(a) - a, ob, a, b, e_rest)
+            e_raw = fields("ac", T.XQ, 0, oa, N // 2, N)
+            fields("ve", T.XQ, 0, oa, 0, N // 2, e_raw)
+            e_pay = species(T.PAY[:, slot0:slot0 + len(rest), 0:pw], c0, 2 * C, M, e_rest)
+            wait("pe", *ev_of["tt"])
+            e_table = unturn(lambda e: B[7][:, e:P // 16:2], lambda o: [((T.QL, T.QH), T.TT[:, 16 * o:P:32]),
+                                                                       ((T.QL63, T.QH63), T.TT[:, 16 * o + 1:P:32])], True)
+            wait("pe", e_raw)
+            e = sig(wrap(B[1][:, 0:N * PIECE], T.E1, T.XQ, 0, M, True, 8))
+            e_new = replace(t - 1, e_sums, new(), e_raw, e_rest, e_first_call)
             wait("ve", e)
-            if CONST_BY != "g":
-                late["rows"] = sig(ve.tensor_scalar(T.ODD[:, 1:2], T.PA[:, 1:2], 1.0, None, A.min))
-            e = link(ve.tensor_scalar(T.LT[:], T.LT[:], 4, P - 1, A.logical_shift_right, A.bitwise_and))
-            wait("ve", e)
-            late["turned"] = sig(ve.tensor_copy(T.UT[:], T.LT[:]))
-        slot(t, 0)
-        if t > 0:
-            e_pay = pay()
-        if not nh:
-            e_head = e_pay
+            e_uh = sig(ve.tensor_copy(T.UH[:], B[1][:, 0:N * PIECE]))
         for i, call in enumerate(calls):
             wait("g", e_pay if i else e_head)
             send(call, "one%d_%d" % (t, i),
-                 lambda q: T.PAY[:, y0 + slot0 + rest.index(q), 0:PIECE] if q in rest else T.HEAD[:, 4 * t + pairs[0].index(q), :],
-                 lambda q: T.PAY[:, y0 + (N + 1) * r, 0:PIECE])
+                 lambda q: T.PAY[:, slot0 + rest.index(q), 0:pw] if q in rest else T.HEAD[:, heads.index(q), 0:pw],
+                 T.PAY[:, y0 + (N + 1) * r, 0:pw])
         if t == 0:
-            if LAW_A < S * S:
-                wait("sy", e_pay)
-                load_law(LAW_A, S * S, e_law)
-            wait("g", e_p2)
-            if CONST_BY == "g":
-                e_pm = sig(g.affine_select(T.PM[:], ident, [[0, 8], [1, 16]], A.not_equal, 0.0, 0, 0))
-                e_p1 = sig(g.affine_select(T.P1[:], T.SW[:], [[0, 8], [1, 16]], A.not_equal, 0.0, -1, 0))
-            e = sig(g.affine_select(T.P2[:], T.P2[:], [[0, 8], [1, 16]], A.is_ge, 0.0, -2, 0))
+            wait("g", e_e1, e_p2, e_id)
+            e_pm = sig(g.affine_select(T.PM[:], ident, [[0, 8], [1, 16]], A.not_equal, 0.0, 0, 0))
+            e_p1 = sig(g.affine_select(T.P1[:], T.SW[:], [[0, 8], [1, 16]], A.not_equal, 0.0, -1, 0))
             e_ef = sig(g.affine_select(T.EF[:], T.E1[:], [[16, 9], [1001, 16]], A.not_equal, float(BASE), -15, -1))
-            wait("g", e)
-            e_p2 = sig(g.affine_select(T.P2[:], T.P2[:], [[16, 8], [1001, 16]], A.not_equal, 1.0, 0, -1))
-            wait("ac", e_ua)
+        if t == 1:
+            last_values(2)
+        wait("ac", e_new if t else ev_of["ua"])
+        e_xa = fields("ac", T.X, xa, oa, 2 if end else 0, N)
+        if end:
+            wait("ve", e_new)
+            fields("ve", T.X, xa, oa, 0, 2, e_xa)
+            e_xb = fields("ac", T.X, xb, ob, 0, N // 2)
+            scatter_last("ve", 2 * M)
         else:
-            wait("ac", e_cooked)
-        n = XA_VE[t]
-        e_xa = fields("ac", T.X, xa, oa, n, N, None)
-        if n:
-            wait("ve", e_cooked if t else e_ua)
-            fields("ve", T.X, xa, oa, 0, n, e_xa)
-        if t == R - 1:
-            wrap_table(TABLE_MM[0])
-        wait("pe", e_xa, e_pay)
-        if JOINT:
-            if t == 0 and CONST_BY != "g":
+            wait("pe", e_xa, e_pay)
+            if t == 0:
                 wait("ac", e_e1)
                 e_e80 = sig(ac.activation(T.E80[:], T.E1[:], F.Copy, scale=float(S)))
-            wait("pe", e_e80, e_head)
-            wrap(B[1][:, 0:W], T.E80, T.X, xa * C, xa * C + M, True, False)
-        else:
-            e_uw = half_wrap(B[0][:, 0:N * PIECE], lambda k: T.X[:, xa * C + k:xa * C + M:8])
-        if t == 0:
-            ramp_end(1)
-            def scaled(out, src, by):
-                if CONST_BY == "ac":
-                    return sig(ac.activation(out, src, F.Copy, scale=by))
-                return sig(ve.tensor_scalar(out, src, by, None, A.mult))
-            if CONST_BY != "g":
-                wait(CONST_BY, e_id, e_sw, late["rows"])
-                e_pm = scaled(T.PM[:], ident, T.ODD[:, 1:2])
-                e_i80 = e_pm if JOINT else scaled(T.I80[:], T.IDW[:], float(S))
-                e_p1 = scaled(T.P1[:], T.SW[:], T.ODD[:, 1:2])
-        e_xb, n = e_raw, XB_FIRST[t]
-        if t > 0:
-            e_xb = new()
-            if n:
-                fields("ac", T.X, xb, ob, 0, n, e_xb)
-        e_uh = e_pay
-        if not JOINT and UH_BY[t] == "ac":
-            wait("ac", e_uw)
-            e_uh = sig(copy("ac", T.UH[:, N * t:N * t + N, :], B[0][:, 0:N * PIECE]))
-        n2 = XB_SECOND[t]
-        if t > 0 and n < n2:
-            fields("ac", T.X, xb, ob, n, n2, e_xb)
-        slot(t, 1)
-        if not JOINT and UH_BY[t] == "ve":
-            wait("ve", e_uw)
-            e_uh = sig(copy("ve", T.UH[:, N * t:N * t + N, :], B[0][:, 0:N * PIECE]))
-
-        def old_firsts(hs):
-            for h in hs:
-                pe.matmul(B[2 + h][:, 0:H], T.PM[:], T.X[:, xa * C + h * H:xa * C + (h + 1) * H], True, False)
-
-        def old_seconds():
-            wait("pe", e_xb)
-            for h in range(2):
-                for i, (a, b) in enumerate(joined(banks[h]) if t else [(s, s + 1) for s in banks[h]]):
-                    src = T.X[:, (xb + a) * C:(xb + b) * C] if t else T.XR[:, order.index(a) * C:order.index(a) * C + C]
-                    pe.matmul(sums(a, b), T.PM[:], src, i == 0, False)
-        wait("pe", e_pm, e_id, e_i80)
-        old_firsts(range(OLD_EARLY[t]))
-        if t == 0:
-            old_seconds()
-        wait("pe", e_uh, e_head)
+            wait("pe", e_e80)
+            wrap(B[1][:, 0:W], T.E80, T.X, xa * C, xa * C + M, False)
+            if t == 0:
+                ramp_end(1)
+            e_xb = fields("ac", T.X, xb, ob, 0, N) if t else e_raw
+            scatter_last("ac", BY_SCALAR[t])
+            scatter(BEFORE[t])
+        wait("pe", e_id, e_pay)
         wait("ve", e_law)
         wait("ac", e_law)
-        e_cols = []
-
-        i0 = W * t
+        e_cols, i0 = [], W * t
         for i, call in enumerate(calls):
-            these, bank, k6 = pairs[i], B[(1, 0, 7)[i]], C // 16
-            strides = [(these[0], these[1] + 1, these[1] - these[0])] if len(these) == 2 else [(a, b, 1) for a, b in joined(these)]
-
-            def add(sel, src, scale, k, first, last):
-                for a, b, step in strides:
-                    j, n3 = these.index(a), len(range(a, b, step))
-                    ins = pe.matmul(bank[:, k6 * j:k6 * (j + n3)], sel, src(scale * a, scale * (b - 1) + 1, scale * step, k),
-                                    first and j == 0, last and b == strides[-1][1])
-                return ins
-            u = lambda a, b, step, k: T.UH[:, N * t + a:N * t + b:step, k:PIECE:2]
-            v = lambda a, b, step, k: T.PAY[:, y0 + a:y0 + b:step, k:PIECE:2]
-            if not JOINT:
-                add(T.I80[:, 8:136], u, 1, 0, True, False)
-                add(T.I80[:, 0:128], u, 1, 1, False, False)
+            these = groups[i]
+            if end:
+                (a, b), bank = these, B[(1, 0, 6)[i]]
+                wait("pe", e_i80, e_uh, ev_of["q"])
+                for k, lo in enumerate([8, 0]):
+                    pe.matmul(bank[:, 0:2 * K6], T.I80[:, lo:lo + 128], T.UH[:, a:b + 1:b - a, k:PIECE:2], k == 0, False)
                 wait("pe", "one%d_%d" % (t, i))
-                add(ident, v, N + 1, 0, False, False)
-                e = sig(add(shift8, v, N + 1, 1, False, True))
-                wait("ve", e)
-                e = sig(ve.tensor_copy(T.IDX[:, i0:i0 + k6 * len(these)], bank[:, 0:k6 * len(these)]))
+                wait("ve", unturn(lambda e: bank[:, e:2 * K6:2], lambda o: [
+                    ((T.QL, T.QH), T.PAY[:, y0 + (N + 1) * a:y0 + (N + 1) * b + 1:(N + 1) * (b - a), o:pw:2])], False))
+                e = sig(ve.tensor_copy(T.IDX[:, i0:i0 + 2 * K6], bank[:, 0:2 * K6]))
             elif i == 0:
                 wait("pe", *["one%d_%d" % (t, j) for j in range(len(calls))])
-                pe.matmul(B[1][:, 0:W], ident, v(0, N * N, N + 1, 0), False, False)
-                e = sig(pe.matmul(B[1][:, 0:W], shift8, v(0, N * N, N + 1, 1), False, True))
-                wait("ve", e)
+                pe.matmul(B[1][:, 0:W], ident, T.PAY[:, y0:y0 + N * N:N + 1, 0:PIECE:2], False, False)
+                wait("ve", sig(pe.matmul(B[1][:, 0:W], shift8, T.PAY[:, y0:y0 + N * N:N + 1, 1:PIECE:2], False, True)))
                 e = sig(ve.tensor_copy(T.IDX[:, i0:i0 + W], B[1][:, 0:W]))
-            ev = new()
-            half = len(these) // 2
-            shares = [("ac", [call[0][0]]), (OWN[t], [r])] if r in these else [("ve", these[:half]), ("ac", these[half:])]
+            ev, half = new(), len(these) // 2
+            shares = [("ac", [near]), ("ve" if t else "ac", [r])] if r in these else [("ve", these[:half]), ("ac", these[half:])]
             for q, ranks in shares:
                 for a, b in joined(ranks):
                     out = T.V[:, v0 + M + a * C:v0 + M + b * C] if a == r else T.COL[:, c0 + a * C:c0 + b * C]
-                    j = W * t + k6 * a if JOINT else i0 + k6 * these.index(a)
+                    j = i0 + K6 * these.index(a) if end else W * t + K6 * a
                     wait(q, e)
-                    ins = copy(q, out, T.LAW[:, 0:S * S].indirect(T.IDX[:, j:j + k6 * (b - a)]))
+                    ins = copy(q, out, T.LAW[:, 0:S * S].indirect(T.IDX[:, j:j + K6 * (b - a)]))
                     if a == r:
                         e_own = sig(ins)
                     else:
                         sig(ins, ev)
-            i0 += k6 * len(these)
+            if i == 0 and not end:
+                scatter(AFTER[t])
+            i0 += K6 * len(these)
             e_cols.append(ev)
             wait("g", ev)
-            send(call, "two%d_%d" % (t, i), lambda q: T.COL[:, c0 + C * q:c0 + C * q + C],
-                 lambda q: T.V[:, v0 + M + C * r:v0 + M + C * r + C])
+            send(call, "two%d_%d" % (t, i), lambda q: T.COL[:, c0 + C * q:c0 + C * q + C], T.V[:, v0 + M + C * r:v0 + M + C * r + C])
         if t == 0:
-            last_columns(VF_CUT, 2 * M)
+            wait("g", sig(g.affine_select(T.P2[:], T.P2[:], [[0, 8], [1, 16]], A.is_ge, 0.0, -2, 0)))
+            e_p2 = sig(g.affine_select(T.P2[:], T.P2[:], [[16, 8], [1001, 16]], A.not_equal, 1.0, 0, -1))
+            ev_of["q"] = new()
+            for sel, base in [(T.QL, -1001), (T.QH, 16)]:
+                sig(g.affine_select(sel[:], T.ONES[:, 0:160], [[-32, 5], [1001, 2], [-1, 16]], A.is_equal, 0.0, base, 1), ev_of["q"])
+            last_values(1)
+        if t == 1:
+            e_i80 = sig(g.affine_select(T.I80[:], T.IDW[:], [[1, 136]], A.not_equal, float(S), -8, -1))
         ready = new()
-        early = t + 1 in looked
-        if early:
-            e_pw = wrap_pointers(t + 1)
-        slot(t, 2)
-        if t == R - 1:
+        if end:
             wait("sy", last[1])
             e_wf = sig(sy.dma_start(T.WF[:], T.TF[0:128:16, :]), n=16)
-        xb_late = t > 0 and max(n, n2) < N
-        if xb_late:
-            wait(XB_BY[t], e_cooked)
-            fields(XB_BY[t], T.X, xb, ob, max(n, n2), N, e_xb)
+            fields("ac", T.X, xb, ob, N // 2, N, e_xb)
+        else:
+            e_pf = new()
+            for side, q in enumerate(["ve", "ac"]):
+                wait(q, last[0])
+                f0, u0 = (2 * t + side) * M, (side * R + t + 1) * W
+                sig(copy(q, T.PF[:, f0:f0 + M], T.TB[:, 0:P].indirect(T.U0[:, u0:u0 + W])), e_pf)
+            last[0] = e_pf
+            if t == 1:
+                wait("ve", ev_of["q"])
+                e = new()
+                for a, b in [(T.QL63, T.QL), (T.QH63, T.QH)]:
+                    sig(ve.tensor_scalar(a[:], b[:], float(BASE), None, A.mult), e)
+                ev_of["tt"] = [sig(ve.transpose(T.TT[:], T.TB[:, 0:P])), e, ev_of["q"]]
+            scatter(END[t])
         mine = T.V[:, v0 + M + C * r:v0 + M + C * r + C]
-        old_firsts(range(OLD_EARLY[t], 2))
-        if t > 0 and not xb_late:
+
+        def old_seconds():
+            wait("pe", e_xb)
+            for ranks, bank, q in banks[t]:
+                for i, (a, b) in enumerate(joined(ranks)):
+                    src = T.X[:, (xb + a) * C:(xb + b) * C] if t else T.XR[:, a * C:b * C]
+                    pe.matmul(sums(t, a, b), T.PM[:], src, i == 0, False)
+        wait("pe", e_pm, e_xa)
+        for h in range(2):
+            pe.matmul(B[2 + h][:, 0:H], T.PM[:], T.X[:, xa * C + h * H:xa * C + (h + 1) * H], True, False)
+        if not end:
             old_seconds()
         wait("pe", e_p1, e_own, *e_cols)
         pe.matmul(B[2 + own][:, C * r - own * H:C * r - own * H + C], T.P1[:], mine, False, False)
@@ -611,45 +451,35 @@ def rank_program(g, core, T, topo):
             for i, (a, b) in enumerate(runs):
                 ins = pe.matmul(B[2 + h][:, a - h * H:b - h * H], T.P1[:], T.COL[:, c0 + a:c0 + b], False, i == len(runs) - 1)
             sig(ins, e_first)
-        p0 = 2 * W * t
-        if t < R - 1 and not early:
-            e_pw = wrap_pointers(t + 1)
-        if xb_late:
+        if end:
             old_seconds()
+        else:
+            wait("pe", e_ef, e_pf)
+            e_pw = sig(wrap(B[6][:, 0:2 * W], T.EF, T.PF, 2 * M * t, 2 * M * (t + 1), True))
         wait("pe", e_p2)
-        pe.matmul(sums(r, r + 1), T.P2[:], mine, False, False)
-        if t < R - 1:
+        pe.matmul(sums(t, r, r + 1), T.P2[:], mine, False, False)
+        if not end:
             wait("ve", e_pw)
             sig(ve.tensor_copy(T.UP[:, p0:p0 + 2 * W], B[6][:, 0:2 * W]), ready)
-        for h, q in enumerate(FIRSTS[t]):
+        for h, q in enumerate(["ac", "ve" if end else "ac"]):
             wait(q, e_first)
             sig(copy(q, T.V[:, v0 + h * H:v0 + (h + 1) * H], B[2 + h][:, 0:H]), ready)
+        if t == 1:
+            scatter_last("ac", BY_SCALAR[2])
 
-    wrap_table(max(TABLE_MM[1], 16))
-    cook = seconds(R - 1)
-    wrap_table(32)
-    e_up = []
-
-    def pointers(h):
-        a, b = h * P // 32, (h + 1) * P // 32
-        wait("ve", e_table[h], e_wf)
-        e = link(ve.tensor_tensor(T.WF[:, a:b], T.WF[:, a:b], B[6 + h][:, 0:P // 32], A.max))
-        wait("ve", e)
-        e_up.append(sig(ve.tensor_scalar(T.UP[:, p0 + a:p0 + b], T.WF[:, a:b], 0.25, None, A.add)))
-    pointers(0)
-    if SECOND_HALF < 0:
-        pointers(1)
-    cooked(R - 1, cook, COOK[0], ready)
-    made = []
-    for i, (a, b) in enumerate(CHUNKS):
+    e_sums = seconds(R - 1)
+    wait("ve", e_table, e_wf)
+    wait("ve", link(ve.tensor_tensor(T.WF[:], T.WF[:], B[7][:, 0:P // 16], A.max)))
+    e_up = sig(ve.tensor_scalar(T.UP[:, p0:p0 + P // 16], T.WF[:], 0.25, None, A.add))
+    replace(R - 1, e_sums, ready)
+    pieces, made = list(zip(CHUNKS, CHUNKS[1:])), []
+    for i, (a, b) in enumerate(pieces):
         q = "ve" if i % 2 == 0 else "ac"
-        if i == SECOND_HALF:
-            pointers(1)
-        wait(q, ready, e_up[(b - 1) * 2 // P])
+        wait(q, ready, e_up)
         made.append(sig(copy(q, T.Y[:, a:b], T.V[:, 0:P + R * 2 * M].indirect(T.UP[:, p0 + a // 16:p0 + b // 16]))))
     e_out = new()
-    for i, (a, b) in enumerate(CHUNKS):
-        q = "ac" if i == len(CHUNKS) - 1 else "sy"
+    for i, (a, b) in enumerate(pieces):
+        q = "ac" if i == len(pieces) - 1 else "sy"
         wait(q, made[i])
         sig(queue[q].dma_start(T.y[:, a:b], T.Y[:, a:b]), e_out, 16)
     wait("g", "left")

from concourse.bass import DstId, RemoteDMATransfer
from concourse.mybir import AluOpType, ActivationFunctionType

N, P, S, C, R = 6, 2048, 80, 96, 3
M = N * C
W = M // 16
H = M // 2
K6 = C // 16
PIECE = C // 8
SLOT = 16
BASE = 63
BLOCK = 8 * BASE
PLANS = [[[0, 1], [2]], [[0, 1], [2]], [[0], [1], [2]]]
FIRST_PIECE, BEFORE, AFTER, END = 256, [1056, 2240], [1152, 2304], [1440, 2304]
BY_SCALAR = [608, 864, 1024]
TF_VALUES = [0, 608, 896, 2 * M]
CHUNKS = [0, 96, 352, 672, 1120, 1632, 2048]

SCRATCH = {
    "V": ("sbuf", [128, P + R * 2 * M], "bfloat16"),
    "LAW": ("sbuf", [128, S * S], "bfloat16"),
    "L": ("sbuf", [128, 2, R * W], "int32"),
    "U0": ("sbuf", [128, 2 * R * W], "uint16"),
    "TB": ("sbuf", [128, P + 2 * M], "bfloat16"),
    "TT": ("sbuf", [128, P], "bfloat16"),
    "K": ("sbuf", [128, H], "bfloat16"),
    "TF": ("sbuf", [128, P], "float32"),
    "VF": ("sbuf", [128, 2 * M], "float32"),
    "WF": ("sbuf", [128, P // 16], "float32"),
    "LT": ("sbuf", [128, 2 * W], "int32"),
    "UT": ("sbuf", [128, 2 * W], "uint16"),
    "IO": ("sbuf", [128, 64], "float32"),
    "MK": ("sbuf", [128, 64], "float32"),
    "PIDX": ("sbuf", [128, 4], "int32"),
    "PA": ("sbuf", [128, 4], "int32"),
    "ODD": ("sbuf", [128, 4], "float32"),
    "ONES": ("sbuf", [128, H], "bfloat16"),
    "XR": ("sbuf", [128, R * M], "bfloat16"),
    "XQ": ("sbuf", [128, M], "bfloat16"),
    "XT": ("sbuf", [128, M], "bfloat16"),
    "X": ("sbuf", [128, R * 2 * M], "bfloat16"),
    "HEAD": ("sbuf", [128, 2, PIECE], "bfloat16"),
    "UH": ("sbuf", [128, N, PIECE], "bfloat16"),
    "PAY": ("sbuf", [128, R * N * N, SLOT], "bfloat16"),
    "IDX": ("sbuf", [128, R * W + 4], "uint16"),
    "COL": ("sbuf", [128, R * M], "bfloat16"),
    "PF": ("sbuf", [128, (R - 1) * 2 * M], "bfloat16"),
    "UP": ("sbuf", [128, (R - 1) * 2 * W + P // 16], "uint16"),
    "Y": ("sbuf", [128, P], "float32"),
}
for _names, _n in [("E1 E80 EF", 144), ("IDW I80", 136), ("PM SW P1 P2", 128), ("QL QH QL63 QH63", 160)]:
    for _name in _names.split():
        SCRATCH[_name] = ("sbuf", [128, _n], "bfloat16")
for _b in range(8):
    SCRATCH["B%d" % _b] = ("psum", [128, 512], "float32")
SEMAPHORES = (["left", "chain", "table"] + ["%s%d_%d" % (s, t, i) for s in ("one", "two") for t in range(R) for i in range(3)]
              + ["s%d" % k for k in range(129)])


def shared_engines(topo, src, dsts):
    eng = [e for e in topo.engines(src, dsts[0]) if all(e in topo.engines(src, d) for d in dsts)]
    n = 1
    while 2 * n <= len(eng):
        n *= 2
    return eng[:n]


def bits(eng):
    return sum(1 << e for e in eng)


def step_calls(topo, cores, r, plan):
    def far(q):
        a, b = topo.chip(cores[r]), topo.chip(cores[q])
        return 0 if a == b else 1 if topo.mates(a, b) else 2 if topo.same_plane(a, b) else 3
    others = [q for q in range(N) if q != r]
    eng = shared_engines(topo, cores[r], [cores[q] for q in others])
    classes = [[q for q in others if far(q) == d] for d in sorted({far(q) for q in others}, reverse=True)]
    calls = []
    for these in plan:
        ranks = [q for i in these for q in classes[i]]
        each = len(eng) // len(ranks)
        calls.append([(q, eng[i * each:(i + 1) * each]) for i, q in enumerate(ranks)])
    return calls


def joined(ranks):
    runs = []
    for q in sorted(ranks):
        if runs and runs[-1][1] == q:
            runs[-1][1] = q + 1
        else:
            runs.append([q, q + 1])
    return runs


def rank_program(g, core, T, topo):
    r = T.rank_of(core)
    if r is None:
        return
    cores = list(T.cores)
    A, F = AluOpType, ActivationFunctionType
    ve, ac, pe, sy = g.vector, g.scalar, g.tensor, g.sync
    queue = {"g": g, "ve": ve, "ac": ac, "pe": pe, "sy": sy}
    total, seen, count = {"chain": 0, "table": 0, "left": 0}, {}, [0]

    def new():
        name = "s%d" % count[0]
        count[0] += 1
        total[name] = 0
        return name

    def sig(ins, ev=None, n=1):
        ev = new() if ev is None else ev
        assert ev not in seen
        ins.then_inc(T.sem[ev], n)
        total[ev] += n
        return ev

    def link(ins, chain="chain"):
        total[chain] += 1
        ins.then_inc(T.sem[chain], 1)
        return (chain, total[chain])

    def wait(q, *evs):
        for ev in evs:
            if q not in seen.setdefault(ev, []):
                seen[ev].append(q)
                name, n = ev if isinstance(ev, tuple) else (ev, total[ev])
                queue[q].wait_ge(T.sem[name], n)

    def copy(q, out, src):
        return ve.tensor_copy(out, src) if q == "ve" else ac.activation(out, src, F.Copy)

    def send(call, sem, src, dst):
        ids = {q: DstId(rid=topo.addr(cores[q])[0], pnc=topo.addr(cores[q])[1]) for q, e in call}
        g.remote_dma_fused([RemoteDMATransfer(dst_ids=[ids[q]], dma_engine_mask=bits(e), remote_sem=T.sem[sem],
                                              src=src(q), dst=dst) for q, e in call], local_sem=T.sem.left)
        total["left"] += sum(len(e) for q, e in call)

    calls_of = [step_calls(topo, cores, r, plan) for plan in PLANS]
    for t in range(R):
        for i in range(len(PLANS[t])):
            total["one%d_%d" % (t, i)] = total["two%d_%d" % (t, i)] = sum(
                len(e) for s in range(N) if s != r for q, e in step_calls(topo, cores, s, PLANS[t])[i] if q == r)
    near = calls_of[0][-1][0][0]
    B = [T["B%d" % b] for b in range(8)]
    ident, shift8 = T.IDW[:, 8:136], T.IDW[:, 0:128]

    def wrap(out, sel, src, lo, hi, stop, n=16):
        for k in range(n):
            ins = pe.matmul(out, sel[:, 16 - k:144 - k], src[:, lo + k:hi:n], k == 0, stop and k == n - 1)
        return ins

    def unturn(out, rows, start):
        todo = [(e, o, sel, src) for e in range(2) for o in range(2) for sel, src in rows(o)]
        for i, (e, o, sel, src) in enumerate(todo):
            lo = 16 + 16 * (e - o)
            ins = pe.matmul(out(e), sel[e][:, lo:lo + 128], src, start and i == 0, i == len(todo) - 1)
        return sig(ins)

    def load_law(k, ev):
        return sig(sy.dma_start(T.LAW[k:128:2, :], T.law[1 - k:128:2, :]), ev, 16)

    values = []

    def last_values(i):
        a, b = TF_VALUES[i:i + 2]
        values.append((a, sig(g.iota(T.VF[:, a:b], [[1, b - a]], P + 4 * M + a, 0, allow_small_or_imprecise_dtypes=True))))

    e_lb = sig(ac.dma_start(T.L[:, 1, :], T.lb[:]), n=16)
    e_fld = sig(sy.dma_start(T.V[:, 0:P], T.fld[:]), n=16)
    e_la = sig(sy.dma_start(T.L[:, 0, :], T.la[:]), n=16)
    e_ones = sig(ve.memset(T.ONES[:], 1.0))
    e_law = load_law(0, None)
    e_pidx = sig(g.iota(T.PIDX[:, 0:1], [[1, 1]], 0, 1))
    e_io = sig(g.iota(T.IO[:], [[1, 64]], 0, 0, allow_small_or_imprecise_dtypes=True))
    wait("g", e_ones)
    e_e1 = sig(g.affine_select(T.E1[:], T.ONES[:, 0:144], [[16, 9], [1001, 16]], A.is_equal, 0.0, -16, -1))
    e_id = sig(g.affine_select(T.IDW[:], T.ONES[:, 0:136], [[1, 136]], A.is_equal, 0.0, -8, -1))
    last_values(0)
    wait("g", sig(g.affine_select(T.SW[:], T.ONES[:, 0:128], [[-2, 64], [1, 2]], A.is_equal, 0.0, -1, 1)))
    e_p2 = sig(g.affine_select(T.P2[:], T.SW[:], [[-2, 64], [1, 2]], A.not_equal, -1.0, -1, 1))
    wait("ac", e_ones)
    e_plus = sig(ac.activation(T.K[:], T.ONES[:], F.Silu, scale=float(2 * M // 64)))

    wait("ve", e_pidx)
    wait("ve", link(ve.tensor_scalar(T.PA[:, 0:1], T.PIDX[:, 0:1], 1, None, A.bitwise_and)))
    wait("ve", link(ve.tensor_copy(T.ODD[:, 0:1], T.PA[:, 0:1])), e_io)
    wait("ve", link(ve.tensor_scalar(T.MK[:], T.IO[:], T.ODD[:, 0:1], None, A.mult)))
    e = link(ve.tensor_tensor(T.TB[:, 0:BASE], T.IO[:, 0:BASE], T.MK[:, 0:BASE], A.subtract))
    for k in (1, 2, 4):
        if k == 2:
            wait("sy", sig(ve.memset(T.WF[:], 0.0)))
            e_tf = sig(sy.dma_start(T.TF[0:128:16, :], T.WF[:]), n=16)
            load_law(1, e_law)
        if k == 4:
            wait("ve", e_lb)
            e_ub = sig(ve.tensor_copy(T.U0[:, R * W:2 * R * W], T.L[:, 1, :]))
        wait("ve", e)
        e = (sig if k == 4 else link)(ve.tensor_scalar(T.TB[:, k * BASE:2 * k * BASE], T.TB[:, 0:k * BASE], T.MK[:, k:k + 1], None, A.add))
    wait("ve", e)
    wait("ac", e)
    e_ramp, ends = new(), []

    def ramp(q, a, b, lo, ev=None):
        out, src, add = T.TB[:, a:b], T.TB[:, lo:lo + b - a], T.MK[:, (a - lo) // BASE:(a - lo) // BASE + 1]
        return sig(ve.tensor_scalar(out, src, add, None, A.add) if q == "ve" else ac.activation(out, src, F.Identity, bias=add), ev)

    def ramp_end(i):
        lo = -(-P // BASE) * BASE
        a = 5 * BLOCK + i * (5 * BLOCK - lo)
        wait("ac", e_ramp)
        ends.append((a - P, ramp("ac", a, min(a + 5 * BLOCK - lo, P + 2 * M), lo)))
    ramp("ve", BLOCK, 2 * BLOCK, 0, e_ramp)

    last, done, ev_of = [e_ramp, e_tf], [0, 0], {}

    def scatter(upto):
        while done[0] < upto:
            i, a = divmod(done[0], M)
            t, side = divmod(i, 2)
            b = min(upto - i * M, M, a + (H if t else M))
            c0 = (side * R + t) * W
            out, src = T.TB[:, 0:P].indirect(T.U0[:, c0 + a // 16:c0 + b // 16]), T.TB[:, P + side * M + a:P + side * M + b]
            wait("ve", ev_of["ua"], e_ub, last[0], *[ev for lo, ev in ends if lo < side * M + b])
            if t == 0:
                last[0] = link(ve.tensor_copy(out, src), "table")
            else:
                wait("ve", e_plus)
                last[0] = link(ve.tensor_tensor(out, src, T.K[:, 0:b - a], A.add), "table")
            done[0] = i * M + b

    def scatter_last(q, upto):
        a = done[1]
        wait(q, last[1], ev_of["ut"], *[ev for lo, ev in values if lo < upto])
        out, src = T.TF[:, 0:P].indirect(T.UT[:, a // 16:upto // 16]), T.VF[:, a:upto]
        last[1] = sig(ve.tensor_copy(out, src) if q == "ve" else ac.activation(out, src, F.Silu))
        done[1] = upto

    far = [[q for q, e in call] for call in calls_of[-1]]
    banks = [[(sorted(far[0] + far[1]), 4, "ac"), (sorted([near, r]), 5, "ve")]] * (R - 1)
    banks.append([(sorted(far[0] + [r]), 4, "ac"), (far[1], 0, "ve"), ([near], 5, "ve")])

    def sums(t, a, b):
        ranks, bank, q = [x for x in banks[t] if a in x[0]][0]
        return B[bank][:, C * ranks.index(a):C * (ranks.index(a) + b - a)]

    def seconds(t):
        v1, evs = P + 2 * M * t + M, []
        for i, call in enumerate(calls_of[t]):
            wait("pe", "two%d_%d" % (t, i))
            runs = joined([q for q, e in call])
            for a, b in runs:
                ins = pe.matmul(sums(t, a, b), T.P2[:], T.V[:, v1 + a * C:v1 + b * C], False, [a, b] == runs[-1])
            evs.append(sig(ins))
        return evs

    def replace(t, evs, ev, *after):
        v1 = P + 2 * M * t + M
        for (ranks, bank, q), e in zip(banks[t], evs):
            wait(q, e, *after)
            for a, b in joined(ranks):
                sig(copy(q, T.V[:, v1 + a * C:v1 + b * C], sums(t, a, b)), ev)
        return ev

    def species(out, x, a, b, ev):
        wait("ve", ev)
        wait("ve", link(ve.transpose(T.XT[:, a:b], T.XR[:, x + a:x + b])))
        return sig(ve.tensor_copy(out, T.XT[:, a:b:16]))

    own = (C * r) // H
    for t in range(R):
        end, calls = t == R - 1, calls_of[t]
        win = T.V[:, 0:P + 2 * M * t]
        xa, xb, c0, v0, y0, p0 = 2 * N * t, 2 * N * t + N, M * t, P + 2 * M * t, N * N * t, 2 * W * t
        groups = [sorted([q for q, e in call] + ([r] if len(call) == 1 else [])) for call in calls]
        heads = groups[0] if end else []
        rest = [s for s in range(N) if s not in heads]
        order, slot0, pw = heads + rest, y0 + (N + 1) * r - rest.index(r), K6 if end else PIECE
        if t == 0:
            off, oa, ob, gate = T.U0, 0, R * W, [e_ub, e_fld]
        else:
            off, oa, ob = T.UP, p0 - 2 * W, p0 - W
            gate = [ready, e_own] + ["two%d_%d" % (t - 1, i) for i in range(len(calls_of[t - 1]))]
            e_sums = seconds(t - 1)

        def fields(q, out, x, o0, a, b, ev=None):
            return sig(copy(q, out[:, (x + a) * C:(x + b) * C], win.indirect(off[:, o0 + a * K6:o0 + b * K6])), ev)

        wait("ac", *gate)
        wait("ve", *gate)
        if not end:
            e_raw = fields("ve", T.XR, N * t, ob, 0, 2 + t)
            fields("ac", T.XR, N * t, ob, 2 + t, N, e_raw)
            if t == 0:
                wait("ve", e_la)
                ev_of["ua"] = sig(ve.tensor_copy(T.U0[:, 0:R * W], T.L[:, 0, :]))
                e = sig(ve.tensor_scalar(T.LT[:], T.L[:, :, (R - 1) * W:R * W], float(P + 1), None, A.mult))
                ramp("ve", 2 * BLOCK, 3 * BLOCK, 0, e_ramp)
                ramp("ac", 4 * BLOCK, 5 * BLOCK, 0, e_ramp)
                wait("ve", e)
                e_lt = link(ve.tensor_scalar(T.LT[:], T.LT[:], 4, P - 1, A.logical_shift_right, A.bitwise_and))
                ramp("ve", 3 * BLOCK, 4 * BLOCK, 0, e_ramp)
            wait("pe", e_e1, e_raw)
            e = sig(wrap(B[0][:, 0:N * PIECE], T.E1, T.XR, c0, c0 + M, True, 8))
            if t > 0:
                e_new = replace(t - 1, e_sums, new(), e_raw)
            wait("ac", e)
            e_head = e_pay = sig(copy("ac", T.PAY[:, slot0:slot0 + N, 0:pw], B[0][:, 0:N * PIECE]))
            if t == 0:
                ramp_end(0)
                scatter(FIRST_PIECE)
                wait("ve", e_lt)
                ev_of["ut"] = sig(ve.tensor_copy(T.UT[:], T.LT[:]))
        else:
            e_first_call, e_rest = new(), new()
            for q, s in zip(["ve", "ac"], heads):
                fields(q, T.XR, N * t + order.index(s) - s, ob, s, s + 1, e_first_call)
            e_head = species(T.HEAD[:, :, 0:pw], c0, 0, 2 * C, e_first_call)
            for a, b in joined(rest):
                fields("ac", T.XR, N * t + order.index(a) - a, ob, a, b, e_rest)
            e_raw = fields("ac", T.XQ, 0, oa, N // 2, N)
            fields("ve", T.XQ, 0, oa, 0, N // 2, e_raw)
            e_pay = species(T.PAY[:, slot0:slot0 + len(rest), 0:pw], c0, 2 * C, M, e_rest)
            wait("pe", *ev_of["tt"])
            e_table = unturn(lambda e: B[7][:, e:P // 16:2], lambda o: [((T.QL, T.QH), T.TT[:, 16 * o:P:32]),
                                                                       ((T.QL63, T.QH63), T.TT[:, 16 * o + 1:P:32])], True)
            wait("pe", e_raw)
            e = sig(wrap(B[1][:, 0:N * PIECE], T.E1, T.XQ, 0, M, True, 8))
            e_new = replace(t - 1, e_sums, new(), e_raw, e_rest, e_first_call)
            wait("ve", e)
            e_uh = sig(ve.tensor_copy(T.UH[:], B[1][:, 0:N * PIECE]))
        for i, call in enumerate(calls):
            wait("g", e_pay if i else e_head)
            send(call, "one%d_%d" % (t, i),
                 lambda q: T.PAY[:, slot0 + rest.index(q), 0:pw] if q in rest else T.HEAD[:, heads.index(q), 0:pw],
                 T.PAY[:, y0 + (N + 1) * r, 0:pw])
        if t == 0:
            wait("g", e_e1, e_p2, e_id)
            e_pm = sig(g.affine_select(T.PM[:], ident, [[0, 8], [1, 16]], A.not_equal, 0.0, 0, 0))
            e_p1 = sig(g.affine_select(T.P1[:], T.SW[:], [[0, 8], [1, 16]], A.not_equal, 0.0, -1, 0))
            e_ef = sig(g.affine_select(T.EF[:], T.E1[:], [[16, 9], [1001, 16]], A.not_equal, float(BASE), -15, -1))
        if t == 1:
            last_values(2)
        wait("ac", e_new if t else ev_of["ua"])
        e_xa = fields("ac", T.X, xa, oa, 2 if end else 0, N)
        if end:
            wait("ve", e_new)
            fields("ve", T.X, xa, oa, 0, 2, e_xa)
            e_xb = fields("ac", T.X, xb, ob, 0, N // 2)
            scatter_last("ve", 2 * M)
        else:
            wait("pe", e_xa, e_pay)
            if t == 0:
                wait("ac", e_e1)
                e_e80 = sig(ac.activation(T.E80[:], T.E1[:], F.Copy, scale=float(S)))
            wait("pe", e_e80)
            wrap(B[1][:, 0:W], T.E80, T.X, xa * C, xa * C + M, False)
            if t == 0:
                ramp_end(1)
            e_xb = fields("ac", T.X, xb, ob, 0, N) if t else e_raw
            scatter_last("ac", BY_SCALAR[t])
            scatter(BEFORE[t])
        wait("pe", e_id, e_pay)
        wait("ve", e_law)
        wait("ac", e_law)
        e_cols, i0 = [], W * t
        for i, call in enumerate(calls):
            these = groups[i]
            if end:
                (a, b), bank = these, B[(1, 0, 6)[i]]
                wait("pe", e_i80, e_uh, ev_of["q"])
                for k, lo in enumerate([8, 0]):
                    pe.matmul(bank[:, 0:2 * K6], T.I80[:, lo:lo + 128], T.UH[:, a:b + 1:b - a, k:PIECE:2], k == 0, False)
                wait("pe", "one%d_%d" % (t, i))
                wait("ve", unturn(lambda e: bank[:, e:2 * K6:2], lambda o: [
                    ((T.QL, T.QH), T.PAY[:, y0 + (N + 1) * a:y0 + (N + 1) * b + 1:(N + 1) * (b - a), o:pw:2])], False))
                e = sig(ve.tensor_copy(T.IDX[:, i0:i0 + 2 * K6], bank[:, 0:2 * K6]))
            elif i == 0:
                wait("pe", *["one%d_%d" % (t, j) for j in range(len(calls))])
                pe.matmul(B[1][:, 0:W], ident, T.PAY[:, y0:y0 + N * N:N + 1, 0:PIECE:2], False, False)
                wait("ve", sig(pe.matmul(B[1][:, 0:W], shift8, T.PAY[:, y0:y0 + N * N:N + 1, 1:PIECE:2], False, True)))
                e = sig(ve.tensor_copy(T.IDX[:, i0:i0 + W], B[1][:, 0:W]))
            ev, half = new(), len(these) // 2
            shares = [("ac", [near]), ("ve" if t else "ac", [r])] if r in these else [("ve", these[:half]), ("ac", these[half:])]
            for q, ranks in shares:
                for a, b in joined(ranks):
                    out = T.V[:, v0 + M + a * C:v0 + M + b * C] if a == r else T.COL[:, c0 + a * C:c0 + b * C]
                    j = i0 + K6 * these.index(a) if end else W * t + K6 * a
                    wait(q, e)
                    ins = copy(q, out, T.LAW[:, 0:S * S].indirect(T.IDX[:, j:j + K6 * (b - a)]))
                    if a == r:
                        e_own = sig(ins)
                    else:
                        sig(ins, ev)
            if i == 0 and not end:
                scatter(AFTER[t])
            i0 += K6 * len(these)
            e_cols.append(ev)
            wait("g", ev)
            send(call, "two%d_%d" % (t, i), lambda q: T.COL[:, c0 + C * q:c0 + C * q + C], T.V[:, v0 + M + C * r:v0 + M + C * r + C])
        if t == 0:
            wait("g", sig(g.affine_select(T.P2[:], T.P2[:], [[0, 8], [1, 16]], A.is_ge, 0.0, -2, 0)))
            e_p2 = sig(g.affine_select(T.P2[:], T.P2[:], [[16, 8], [1001, 16]], A.not_equal, 1.0, 0, -1))
            ev_of["q"] = new()
            for sel, base in [(T.QL, -1001), (T.QH, 16)]:
                sig(g.affine_select(sel[:], T.ONES[:, 0:160], [[-32, 5], [1001, 2], [-1, 16]], A.is_equal, 0.0, base, 1), ev_of["q"])
            last_values(1)
        if t == 1:
            e_i80 = sig(g.affine_select(T.I80[:], T.IDW[:], [[1, 136]], A.not_equal, float(S), -8, -1))
        ready = new()
        if end:
            wait("sy", last[1])
            e_wf = sig(sy.dma_start(T.WF[:], T.TF[0:128:16, :]), n=16)
            fields("ac", T.X, xb, ob, N // 2, N, e_xb)
        else:
            e_pf = new()
            for side, q in enumerate(["ve", "ac"]):
                wait(q, last[0])
                f0, u0 = (2 * t + side) * M, (side * R + t + 1) * W
                sig(copy(q, T.PF[:, f0:f0 + M], T.TB[:, 0:P].indirect(T.U0[:, u0:u0 + W])), e_pf)
            last[0] = e_pf
            if t == 1:
                wait("ve", ev_of["q"])
                e = new()
                for a, b in [(T.QL63, T.QL), (T.QH63, T.QH)]:
                    sig(ve.tensor_scalar(a[:], b[:], float(BASE), None, A.mult), e)
                ev_of["tt"] = [sig(ve.transpose(T.TT[:], T.TB[:, 0:P])), e, ev_of["q"]]
            scatter(END[t])
        mine = T.V[:, v0 + M + C * r:v0 + M + C * r + C]

        def old_seconds():
            wait("pe", e_xb)
            for ranks, bank, q in banks[t]:
                for i, (a, b) in enumerate(joined(ranks)):
                    src = T.X[:, (xb + a) * C:(xb + b) * C] if t else T.XR[:, a * C:b * C]
                    pe.matmul(sums(t, a, b), T.PM[:], src, i == 0, False)
        wait("pe", e_pm, e_xa)
        for h in range(2):
            pe.matmul(B[2 + h][:, 0:H], T.PM[:], T.X[:, xa * C + h * H:xa * C + (h + 1) * H], True, False)
        if not end:
            old_seconds()
        wait("pe", e_p1, e_own, *e_cols)
        pe.matmul(B[2 + own][:, C * r - own * H:C * r - own * H + C], T.P1[:], mine, False, False)
        e_first = new()
        for h in range(2):
            runs = [(h * H, (h + 1) * H)]
            if h == own:
                runs = [(a, b) for a, b in [(h * H, C * r), (C * r + C, (h + 1) * H)] if a < b]
            for i, (a, b) in enumerate(runs):
                ins = pe.matmul(B[2 + h][:, a - h * H:b - h * H], T.P1[:], T.COL[:, c0 + a:c0 + b], False, i == len(runs) - 1)
            sig(ins, e_first)
        if end:
            old_seconds()
        else:
            wait("pe", e_ef, e_pf)
            e_pw = sig(wrap(B[6][:, 0:2 * W], T.EF, T.PF, 2 * M * t, 2 * M * (t + 1), True))
        wait("pe", e_p2)
        pe.matmul(sums(t, r, r + 1), T.P2[:], mine, False, False)
        if not end:
            wait("ve", e_pw)
            sig(ve.tensor_copy(T.UP[:, p0:p0 + 2 * W], B[6][:, 0:2 * W]), ready)
        for h, q in enumerate(["ac", "ve" if end else "ac"]):
            wait(q, e_first)
            sig(copy(q, T.V[:, v0 + h * H:v0 + (h + 1) * H], B[2 + h][:, 0:H]), ready)
        if t == 1:
            scatter_last("ac", BY_SCALAR[2])

    e_sums = seconds(R - 1)
    wait("ve", e_table, e_wf)
    wait("ve", link(ve.tensor_tensor(T.WF[:], T.WF[:], B[7][:, 0:P // 16], A.max)))
    e_up = sig(ve.tensor_scalar(T.UP[:, p0:p0 + P // 16], T.WF[:], 0.25, None, A.add))
    replace(R - 1, e_sums, ready)
    pieces, made = list(zip(CHUNKS, CHUNKS[1:])), []
    for i, (a, b) in enumerate(pieces):
        q = "ve" if i % 2 == 0 else "ac"
        wait(q, ready, e_up)
        made.append(sig(copy(q, T.Y[:, a:b], T.V[:, 0:P + R * 2 * M].indirect(T.UP[:, p0 + a // 16:p0 + b // 16]))))
    e_out = new()
    for i, (a, b) in enumerate(pieces):
        q = "ac" if i == len(pieces) - 1 else "sy"
        wait(q, made[i])
        sig(queue[q].dma_start(T.y[:, a:b], T.Y[:, a:b]), e_out, 16)
    wait("g", "left")
    wait("g", *[ev for ev in total if ev not in seen and ev not in (e_out, "chain", "table")])
    wait("sy", e_out)
